import numpy as np
import ml_dtypes


def mxq(x, axis, fmt="e4m3"):
    dtype, down = {"e4m3": (ml_dtypes.float8_e4m3fn, 7), "e5m2": (ml_dtypes.float8_e5m2, 14)}[fmt]
    v = np.moveaxis(np.asarray(x, np.float32).astype(ml_dtypes.bfloat16).astype(np.float64), axis, -1)
    blocks = v.reshape(v.shape[:-1] + (-1, 32))
    amax = np.abs(blocks).max(-1, keepdims=True)
    byte = np.maximum(np.where(amax > 0, np.frexp(amax)[1] - 1 + 127, 0) - down, 1)
    scale = np.exp2(byte - 127.0)
    codes = (blocks / scale).astype(np.float32).astype(dtype).astype(np.float64)
    return np.moveaxis((codes * scale).reshape(v.shape), -1, axis)


WIDE = False


def mx_kscale(k):
    if not WIDE:
        return np.ones(k)
    levels = np.array([10, -10, 5, -5, 0])
    if k % 512:
        return np.exp2(np.random.permutation(np.resize(levels, k // 32))).repeat(32)
    a = np.empty((k // 512, 16))
    for p in range(k // 512):
        a[p, :8] = np.random.permutation(np.resize(levels, 8))
        for g in range(8):
            far = levels[np.abs(levels - a[p, g]) >= 10]
            a[p, g + 8] = far[np.random.randint(len(far))]
    return np.exp2(a.ravel()).repeat(32)


def f64(x):
    return np.asarray(x).astype(np.float64)


def striped(idx):
    return np.tile(idx.reshape(-1, 16).T, (8, 1)).astype(np.uint16)


def unstriped(offs):
    return offs[:16].T.reshape(-1).astype(np.int64)


E2M1 = np.array([0.0, 0.5, 1.0, 1.5, 2.0, 3.0, 4.0, 6.0, -0.0, -0.5, -1.0, -1.5, -2.0, -3.0, -4.0, -6.0])


def pack_weight(w, fmt):
    k, n = w.shape
    w = f64(np.asarray(w, np.float32).astype(ml_dtypes.bfloat16)).reshape(k // 32, 32, n)
    amax = np.abs(w).max(1)
    if fmt == "e4m3":
        byte = np.frexp(amax)[1] - 1 + 127 - 7
    else:
        mant, ex = np.frexp(amax / 6.0)
        byte = np.where(mant > 0.5, ex, ex - 1) + 127
    byte = np.clip(np.where(amax > 0, byte, 1), 1, 254)
    scaled = (w * np.exp2(127.0 - byte)[:, None, :]).reshape(k, n).astype(np.float32)
    by_word = np.ascontiguousarray(scaled.reshape(k // 512, 128, 4, n).transpose(0, 1, 3, 2))
    if fmt == "e4m3":
        words = by_word.astype(ml_dtypes.float8_e4m3fn).view(np.uint8)
    else:
        c = by_word.astype(ml_dtypes.float4_e2m1fn).view(np.uint8) & 0xF
        words = (c[..., 0::2] | (c[..., 1::2] << 4)).reshape(k // 512, 128, 2 * n)
    return np.ascontiguousarray(words), np.ascontiguousarray(byte.astype(np.uint8).reshape(k // 512, 16, n))


def unpack_weight(words, scales, fmt):
    g, _, n = scales.shape
    words = np.ascontiguousarray(words).reshape(g, 128, n, -1)
    if fmt == "e4m3":
        vals = words.view(ml_dtypes.float8_e4m3fn).astype(np.float64)
    else:
        nib = np.empty((g, 128, n, 4), np.uint8)
        nib[..., 0::2] = words & 0xF
        nib[..., 1::2] = words >> 4
        vals = E2M1[nib]
    vals = vals * np.repeat(np.exp2(scales.astype(np.float64) - 127.0), 8, axis=1)[..., None]
    return vals.transpose(0, 1, 3, 2).reshape(g * 512, n)


def relu2(v):
    return np.maximum(v, 0.0) ** 2


K, T, E, C, H, N = 512, 512, 2, 256, 512, 512


def by_expert(wq, xq):
    return np.concatenate([wq[e].T @ xq[:, e * C:(e + 1) * C] for e in range(E)], axis=1)


def setup_inputs():
    n = np.random.standard_normal
    s = mx_kscale(K)[:, None]
    u = mx_kscale(H)
    w1 = [pack_weight(m, "e2m1") for m in n((E, K, H)) / np.sqrt(K) / s[None] * u[None, None, :]]
    w2 = [pack_weight(m, "e2m1") for m in n((E, H, N)) / np.sqrt(H) / u[None, :, None] ** 2]
    return {
        "xT": (n((K, T)) * s).astype(np.float32),
        "w1_words": np.stack([m[0] for m in w1]),
        "w1_scales": np.stack([m[1] for m in w1]),
        "w2_words": np.stack([m[0] for m in w2]),
        "w2_scales": np.stack([m[1] for m in w2]),
        "gate": np.tile(np.random.uniform(0.2, 1.0, E * C), (N, 1)).astype(np.float32),
        "offs": striped(np.random.permutation(T)[:E * C]),
        "dst": striped(np.random.permutation(T)[:E * C]),
    }


def reference(xT, w1_words, w1_scales, w2_words, w2_scales, gate, offs, dst):
    idx = unstriped(offs)
    w1 = np.stack([unpack_weight(w1_words[e], w1_scales[e], "e2m1") for e in range(E)])
    w2 = np.stack([unpack_weight(w2_words[e], w2_scales[e], "e2m1") for e in range(E)])
    xq = mxq(f64(xT)[:, idx], 0, "e4m3")
    h = relu2(by_expert(w1, xq))
    y = by_expert(w2, mxq(h, 0, "e4m3"))
    out = np.zeros((N, T))
    out[:, unstriped(dst)] = f64(gate) * y
    return out

@@ -1,0 +1,221 @@
+from contextlib import ExitStack
+
+import concourse.mybir as mybir
+
+F32 = mybir.dt.float32
+BF16 = mybir.dt.bfloat16
+I32 = mybir.dt.int32
+U32 = mybir.dt.uint32
+U16 = mybir.dt.uint16
+U8 = mybir.dt.uint8
+FP8X4 = mybir.dt.float8_e4m3fn_x4
+FP4X4 = mybir.dt.float4_e2m1fn_x4
+MULT = mybir.AluOpType.mult
+RELU = mybir.ActivationFunctionType.Relu
+SQUARE = mybir.ActivationFunctionType.Square
+
+P = 128
+K, T, E, C, H, N = 512, 512, 2, 256, 512, 512
+X_CHUNKS = ((0, 384), (384, 512))
+UNITS = ((0, 0, 128), (0, 128, 256), (1, 0, 256))
+W0 = 128
+FLOPS = 2 * E * C * H * (K + N)
+
+
+def tile_moe_two_mlp_relu2_kernel(tc, xT, w1_words, w1_scales, w2_words, w2_scales, gate, offs, dst, out):
+    nc = tc.nc
+    with ExitStack() as ctx:
+        keep = ctx.enter_context(tc.tile_pool(name="keep", bufs=1))
+        psum = ctx.enter_context(tc.psum_pool(name="psum", bufs=1))
+
+        offs_t = keep.tile([P, T // 16], U16, name="offs_t")
+        dst_t = keep.tile([P, T // 16], U16, name="dst_t")
+        s1_raw = keep.tile([P, E, H], U8, name="s1_raw", align_bytes=64)
+        s2 = keep.tile([P, E, N], U8, name="s2", align_bytes=64)
+        xs = keep.tile([P, T], U8, name="xs", align_bytes=64)
+        xw = keep.tile([P, T], U32, name="xw", align_bytes=64)
+        warm = keep.tile([P, 1], F32, name="warm")
+        w1_raw = keep.tile([P, E, 2 * H], U8, name="w1_raw", align_bytes=64)
+        w2 = keep.tile([P, E, 2 * N], U8, name="w2", align_bytes=64)
+        x_raw = [keep.tile([P, 4, b - a], F32, name=f"x_raw{a}", tag=f"slot{a}", align_bytes=64) for a, b in X_CHUNKS]
+        gate_t = keep.tile([P, E * C], F32, name="gate_t")
+
+        nc.vector.memset(s1_raw[:].rearrange("p e i -> p (e i)").bitcast(I32), 0)
+        nc.vector.memset(s2[:].rearrange("p e i -> p (e i)").bitcast(I32), 0)
+        nc.vector.memset(warm[:], 0.0)
+        nc.scalar.activation(warm[:], warm[:], SQUARE)
+
+        x_rows = xT.rearrange("(p j) w -> p j w", j=4)
+        for q in range(4):
+            nc.scalar.dma_start(
+                s1_raw[32 * q : 32 * q + 4].bitcast(I32),
+                w1_scales[:, 0, 4 * q : 4 * q + 4, :].rearrange("e q i -> q e i").bitcast(I32),
+            )
+        nc.sync.dma_start(offs_t[:], offs)
+        nc.sync.dma_start(w1_raw[:, 0, :].bitcast(I32), w1_words[0, 0].bitcast(I32))
+        for i, (a, b) in enumerate(X_CHUNKS):
+            nc.sync.dma_start(x_raw[i][:], x_rows[:, :, a:b])
+        nc.gpsimd.memset(xs[:], 0)
+        nc.sync.dma_start(w1_raw[:, 1, :].bitcast(I32), w1_words[1, 0].bitcast(I32))
+        for q in range(4):
+            nc.sync.dma_start(
+                s2[32 * q : 32 * q + 4].bitcast(I32),
+                w2_scales[:, 0, 4 * q : 4 * q + 4, :].rearrange("e q i -> q e i").bitcast(I32),
+            )
+        nc.sync.dma_start(w2[:].bitcast(I32), w2_words[:, 0].rearrange("e p b -> p e b").bitcast(I32))
+        nc.sync.dma_start(gate_t[:], gate[0:P, :])
+        nc.sync.dma_start(dst_t[:], dst)
+
+        def permute_words(e, dest):
+            nc.vector.tensor_copy(
+                dest[:].bitcast(U16).rearrange("p (t m) -> p t m", t=4),
+                w1_raw[:, e, :].bitcast(U16).rearrange("p (m t) -> p t m", t=4),
+            )
+
+        def permute_scales(e, dest):
+            nc.vector.tensor_copy(
+                dest[:].rearrange("p (t m) -> p t m", t=4),
+                s1_raw[:, e, :].rearrange("p (m t) -> p t m", t=4),
+            )
+
+        w1 = [keep.tile([P, 2 * H], U8, name="w1_0", align_bytes=64)]
+        permute_words(0, w1[0])
+
+        x_grp = [keep.tile([P, 256, 4], BF16, name=f"x_grp{i}", tag=f"grp{i}", align_bytes=64) for i in range(2)]
+
+        def group(i, a, b, engine):
+            c0 = X_CHUNKS[i][0]
+            src = x_raw[i][:, :, a - c0 : b - c0].rearrange("p j w -> p w j")
+            dest = x_grp[a // 256][:, a % 256 : (b - 1) % 256 + 1, :]
+            if engine == "s":
+                nc.scalar.copy(dest, src)
+            else:
+                nc.vector.tensor_copy(dest, src)
+
+        def quantize_x(i):
+            cols = slice(256 * i, 256 * (i + 1))
+            nc.vector.quantize_mx(
+                out=xw[:, cols].bitcast(FP8X4), scales=xs[:, cols], in_=x_grp[i][:].rearrange("p w j -> p (w j)")
+            )
+
+        group(0, 0, 176, "v")
+        group(0, 176, 256, "s")
+        quantize_x(0)
+        group(0, 256, 320, "s")
+        group(0, 320, 384, "v")
+        group(1, 384, 432, "s")
+        group(1, 432, 512, "v")
+        quantize_x(1)
+        s1 = [keep.tile([P, H], U8, name="s1_0", tag="grp0", align_bytes=64)]
+        permute_scales(0, s1[0])
+
+        gw = [keep.tile([P, C], U32, name=f"gw{e}", align_bytes=64) for e in range(E)]
+        gs = [keep.tile([P, C], U8, name=f"gs{e}", align_bytes=64) for e in range(E)]
+        a_ps, y_ps, r, h_grp, hw, hs, y_sb = [], [], [], [], [], [], []
+        banks = [psum.tile([P, 512], F32, name=f"bank{i}") for i in range(6)]
+        a_banks = ((0,), (0,), (0, 1))
+        a_hi = banks[4][:].rearrange("p (t s) -> p t s", s=W0)
+        y_first = banks[5][:].rearrange("p (t s) -> p t s", s=W0)
+        y_banks = ((1,), (1,), (2, 3))
+        for u, (e, a, b) in enumerate(UNITS):
+            w = b - a
+            a_ps.append([banks[i][:].rearrange("p (t s) -> p t s", s=w) for i in a_banks[u]])
+            y_ps.append([banks[i][:].rearrange("p (t s) -> p t s", s=w) for i in y_banks[u]])
+            r.append(keep.tile([P, 4, w], F32, name=f"r{u}", align_bytes=64))
+            h_grp.append(keep.tile([P, w, 4], BF16, name=f"h_grp{u}", align_bytes=64))
+            hw.append(keep.tile([P, w], U32, name=f"hw{u}", align_bytes=64))
+            hs.append(keep.tile([P, w], U8, name=f"hs{u}", align_bytes=64))
+            y_sb.append(keep.tile([P, 4, w], F32, name=f"y_sb{u}"))
+        win = [keep.tile([P, T], F32, name=f"win{b}") for b in range(4)]
+
+        def gather(u):
+            e, a, b = UNITS[u]
+            lst = offs_t[:, (e * C + a) // 16 : (e * C + b) // 16]
+            nc.vector.tensor_copy(gw[e][:, a:b], xw[:].indirect(lst))
+            nc.vector.tensor_copy(gs[e][:, a:b], xs[:].indirect(lst))
+
+        def first(u):
+            e, a, b = UNITS[u]
+            n = 512 // (b - a)
+            for t in range(4):
+                nc.tensor.matmul_mx(
+                    out=(a_hi if u == 0 and t >= 2 else a_ps[u][t // n])[:, t % n, :],
+                    lhsT=w1[e][:, 256 * t : 256 * (t + 1)].bitcast(FP4X4),
+                    lhsT_scale=s1[e][:, P * t : P * (t + 1)],
+                    rhs=gw[e][:, a:b].bitcast(FP8X4),
+                    rhs_scale=gs[e][:, a:b],
+                    start=True,
+                    stop=True,
+                )
+
+        def hidden(u):
+            e, a, b = UNITS[u]
+            n = 512 // (b - a)
+            if u == 0:
+                nc.scalar.activation(r[u][:, 0:2, :], a_ps[u][0][:, 0:2, :], RELU)
+                nc.scalar.activation(r[u][:, 2:4, :], a_hi[:, 2:4, :], RELU)
+            else:
+                for i, bank in enumerate(a_ps[u]):
+                    nc.scalar.activation(r[u][:, i * n : (i + 1) * n, :], bank, RELU)
+            for c in range(0, b - a, 128):
+                nc.scalar.activation(
+                    h_grp[u][:, c : c + 128, :], r[u][:, :, c : c + 128].rearrange("p t s -> p s t"), SQUARE
+                )
+            nc.vector.quantize_mx(
+                out=hw[u][:].bitcast(FP8X4), scales=hs[u][:], in_=h_grp[u][:].rearrange("p s t -> p (s t)")
+            )
+
+        def second(u):
+            e, a, b = UNITS[u]
+            n = 512 // (b - a)
+            for i in range(4):
+                nc.tensor.matmul_mx(
+                    out=(y_first if u == 0 and i == 0 else y_ps[u][i // n])[:, i % n, :],
+                    lhsT=w2[:, e, 256 * i : 256 * (i + 1)].bitcast(FP4X4),
+                    lhsT_scale=s2[:, e, P * i : P * (i + 1)],
+                    rhs=hw[u][:].bitcast(FP8X4),
+                    rhs_scale=hs[u][:],
+                    start=True,
+                    stop=True,
+                )
+            if u == 0:
+                nc.scalar.copy(y_sb[u][:, 0, :], y_first[:, 0, :])
+                nc.scalar.copy(y_sb[u][:, 1:4, :], y_ps[u][0][:, 1:4, :])
+            else:
+                for i, bank in enumerate(y_ps[u]):
+                    nc.scalar.copy(y_sb[u][:, i * n : (i + 1) * n, :], bank)
+
+        def scatter(u, i):
+            e, a, b = UNITS[u]
+            nc.vector.tensor_tensor(
+                win[i][:].indirect(dst_t[:, (e * C + a) // 16 : (e * C + b) // 16]),
+                y_sb[u][:, i, :],
+                gate_t[:, e * C + a : e * C + b],
+                MULT,
+            )
+            if u == len(UNITS) - 1:
+                nc.sync.dma_start(out[i * P : (i + 1) * P, :], win[i][:])
+
+        gather(0)
+        first(0)
+        hidden(0)
+        gather(1)
+        first(1)
+        second(0)
+        gather(2)
+        w1.append(keep.tile([P, 2 * H], U8, name="w1_1", tag="grp1", align_bytes=64))
+        s1.append(keep.tile([P, H], U8, name="s1_1", tag="slot384", align_bytes=64))
+        permute_words(1, w1[1])
+        permute_scales(1, s1[1])
+        scatter(0, 0)
+        hidden(1)
+        first(2)
+        hidden(2)
+        for i in range(1, 4):
+            scatter(0, i)
+        second(1)
+        for i in range(4):
+            scatter(1, i)
+        second(2)
+        for i in range(4):
+            scatter(2, i)

@@ -16,8 +16,7 @@ SQUARE = mybir.ActivationFunctionType.Square
 
 P = 128
 K, T, E, C, H, N = 512, 512, 2, 256, 512, 512
-X_CHUNKS = ((0, 384), (384, 512))
-UNITS = ((0, 0, 128), (0, 128, 256), (1, 0, 256))
+UNITS = ((0, 128), (128, 256), (256, 512))
 W0 = 128
 FLOPS = 2 * E * C * H * (K + N)
 
@@ -26,43 +25,45 @@ def tile_moe_two_mlp_relu2_kernel(tc, xT, w1_words, w1_scales, w2_words, w2_scal
     nc = tc.nc
     with ExitStack() as ctx:
         keep = ctx.enter_context(tc.tile_pool(name="keep", bufs=1))
+        shared = ctx.enter_context(tc.tile_pool(name="shared", bufs=1))
         psum = ctx.enter_context(tc.psum_pool(name="psum", bufs=1))
 
         offs_t = keep.tile([P, T // 16], U16, name="offs_t")
         dst_t = keep.tile([P, T // 16], U16, name="dst_t")
         s1_raw = keep.tile([P, E, H], U8, name="s1_raw", align_bytes=64)
         s2 = keep.tile([P, E, N], U8, name="s2", align_bytes=64)
-        xs = keep.tile([P, T], U8, name="xs", align_bytes=64)
-        xw = keep.tile([P, T], U32, name="xw", align_bytes=64)
         warm = keep.tile([P, 1], F32, name="warm")
         w1_raw = keep.tile([P, E, 2 * H], U8, name="w1_raw", align_bytes=64)
         w2 = keep.tile([P, E, 2 * N], U8, name="w2", align_bytes=64)
-        x_raw = [keep.tile([P, 4, b - a], F32, name=f"x_raw{a}", tag=f"slot{a}", align_bytes=64) for a, b in X_CHUNKS]
+        x_raw = [
+            keep.tile([P, 2, T], F32, name="x_raw0", align_bytes=64),
+            keep.tile([P, 2, T], F32, name="x_raw1", align_bytes=64),
+        ]
         gate_t = keep.tile([P, E * C], F32, name="gate_t")
 
-        nc.vector.memset(s1_raw[:].rearrange("p e i -> p (e i)").bitcast(I32), 0)
-        nc.vector.memset(s2[:].rearrange("p e i -> p (e i)").bitcast(I32), 0)
+        nc.gpsimd.memset(s1_raw[:].rearrange("p e i -> p (e i)").bitcast(I32), 0)
         nc.vector.memset(warm[:], 0.0)
-        nc.scalar.activation(warm[:], warm[:], SQUARE)
+        nc.vector.memset(s2[:].rearrange("p e i -> p (e i)").bitcast(I32), 0)
 
         x_rows = xT.rearrange("(p j) w -> p j w", j=4)
         for q in range(4):
-            nc.scalar.dma_start(
+            (nc.scalar if q < 3 else nc.gpsimd).dma_start(
                 s1_raw[32 * q : 32 * q + 4].bitcast(I32),
                 w1_scales[:, 0, 4 * q : 4 * q + 4, :].rearrange("e q i -> q e i").bitcast(I32),
             )
+        nc.scalar.activation(warm[:], warm[:], SQUARE)
         nc.sync.dma_start(offs_t[:], offs)
         nc.sync.dma_start(w1_raw[:, 0, :].bitcast(I32), w1_words[0, 0].bitcast(I32))
-        for i, (a, b) in enumerate(X_CHUNKS):
-            nc.sync.dma_start(x_raw[i][:], x_rows[:, :, a:b])
-        nc.gpsimd.memset(xs[:], 0)
+        nc.sync.dma_start(x_raw[0][:], x_rows[:, 0:2, :])
+        nc.sync.dma_start(x_raw[1][:, 0, :], x_rows[:, 2, :])
+        nc.sync.dma_start(x_raw[1][:, 1, :], x_rows[:, 3, :])
         nc.sync.dma_start(w1_raw[:, 1, :].bitcast(I32), w1_words[1, 0].bitcast(I32))
+        nc.sync.dma_start(w2[:].bitcast(I32), w2_words[:, 0].rearrange("e p b -> p e b").bitcast(I32))
         for q in range(4):
             nc.sync.dma_start(
                 s2[32 * q : 32 * q + 4].bitcast(I32),
                 w2_scales[:, 0, 4 * q : 4 * q + 4, :].rearrange("e q i -> q e i").bitcast(I32),
             )
-        nc.sync.dma_start(w2[:].bitcast(I32), w2_words[:, 0].rearrange("e p b -> p e b").bitcast(I32))
         nc.sync.dma_start(gate_t[:], gate[0:P, :])
         nc.sync.dma_start(dst_t[:], dst)
 
@@ -78,144 +79,185 @@ def tile_moe_two_mlp_relu2_kernel(tc, xT, w1_words, w1_scales, w2_words, w2_scal
                 s1_raw[:, e, :].rearrange("p (m t) -> p t m", t=4),
             )
 
-        w1 = [keep.tile([P, 2 * H], U8, name="w1_0", align_bytes=64)]
+        w1 = [
+            keep.tile([P, 2 * H], U8, name="w1_0", align_bytes=64),
+            keep.tile([P, 2 * H], U8, name="w1_1", align_bytes=64),
+        ]
+        s1 = [
+            keep.tile([P, H], U8, name="s1_0", align_bytes=64),
+            keep.tile([P, H], U8, name="s1_1", align_bytes=64),
+        ]
         permute_words(0, w1[0])
-
-        x_grp = [keep.tile([P, 256, 4], BF16, name=f"x_grp{i}", tag=f"grp{i}", align_bytes=64) for i in range(2)]
-
-        def group(i, a, b, engine):
-            c0 = X_CHUNKS[i][0]
-            src = x_raw[i][:, :, a - c0 : b - c0].rearrange("p j w -> p w j")
-            dest = x_grp[a // 256][:, a % 256 : (b - 1) % 256 + 1, :]
-            if engine == "s":
-                nc.scalar.copy(dest, src)
-            else:
-                nc.vector.tensor_copy(dest, src)
-
-        def quantize_x(i):
-            cols = slice(256 * i, 256 * (i + 1))
-            nc.vector.quantize_mx(
-                out=xw[:, cols].bitcast(FP8X4), scales=xs[:, cols], in_=x_grp[i][:].rearrange("p w j -> p (w j)")
-            )
-
-        group(0, 0, 176, "v")
-        group(0, 176, 256, "s")
-        quantize_x(0)
-        group(0, 256, 320, "s")
-        group(0, 320, 384, "v")
-        group(1, 384, 432, "s")
-        group(1, 432, 512, "v")
-        quantize_x(1)
-        s1 = [keep.tile([P, H], U8, name="s1_0", tag="grp0", align_bytes=64)]
         permute_scales(0, s1[0])
 
-        gw = [keep.tile([P, C], U32, name=f"gw{e}", align_bytes=64) for e in range(E)]
-        gs = [keep.tile([P, C], U8, name=f"gs{e}", align_bytes=64) for e in range(E)]
-        a_ps, y_ps, r, h_grp, hw, hs, y_sb = [], [], [], [], [], [], []
-        banks = [psum.tile([P, 512], F32, name=f"bank{i}") for i in range(6)]
-        a_banks = ((0,), (0,), (0, 1))
-        a_hi = banks[4][:].rearrange("p (t s) -> p t s", s=W0)
-        y_first = banks[5][:].rearrange("p (t s) -> p t s", s=W0)
-        y_banks = ((1,), (1,), (2, 3))
-        for u, (e, a, b) in enumerate(UNITS):
-            w = b - a
-            a_ps.append([banks[i][:].rearrange("p (t s) -> p t s", s=w) for i in a_banks[u]])
-            y_ps.append([banks[i][:].rearrange("p (t s) -> p t s", s=w) for i in y_banks[u]])
-            r.append(keep.tile([P, 4, w], F32, name=f"r{u}", align_bytes=64))
-            h_grp.append(keep.tile([P, w, 4], BF16, name=f"h_grp{u}", align_bytes=64))
-            hw.append(keep.tile([P, w], U32, name=f"hw{u}", align_bytes=64))
-            hs.append(keep.tile([P, w], U8, name=f"hs{u}", align_bytes=64))
-            y_sb.append(keep.tile([P, 4, w], F32, name=f"y_sb{u}"))
-        win = [keep.tile([P, T], F32, name=f"win{b}") for b in range(4)]
+        pairs = [keep.tile([P, T, 2], BF16, name=f"pairs{i}", align_bytes=64) for i in range(2)]
 
-        def gather(u):
-            e, a, b = UNITS[u]
-            lst = offs_t[:, (e * C + a) // 16 : (e * C + b) // 16]
-            nc.vector.tensor_copy(gw[e][:, a:b], xw[:].indirect(lst))
-            nc.vector.tensor_copy(gs[e][:, a:b], xs[:].indirect(lst))
+        def pair_up(i):
+            nc.scalar.copy(
+                pairs[i][:].rearrange("p (c i) j -> p c j i", i=4),
+                x_raw[i][:].rearrange("p j (c i) -> p c j i", i=4),
+            )
+
+        rest = T - W0
+        xg = [
+            shared.tile([P, 128, 4], BF16, name="xg0", align_bytes=64, offset=16384),
+            shared.tile([P, 128, 4], BF16, name="xg1", align_bytes=64, offset=12864),
+            shared.tile([P, 256, 4], BF16, name="xg2", align_bytes=64, offset=10304),
+        ]
+        gp = shared.tile([P, 2, rest], U32, name="gp", align_bytes=64, offset=16384)
+        h_grp = [
+            keep.tile([P, 128, 4], BF16, name="h_grp0", align_bytes=64),
+            keep.tile([P, 128, 4], BF16, name="h_grp1", align_bytes=64),
+            keep.tile([P, 256, 4], BF16, name="h_grp2", align_bytes=64),
+        ]
+        gw = [keep.tile([P, b - a], U32, name=f"gw{u}", align_bytes=64) for u, (a, b) in enumerate(UNITS)]
+        win = [
+            keep.tile([P, T], F32, name="win0"),
+            keep.tile([P, T], F32, name="win1"),
+            keep.tile([P, T], F32, name="win2"),
+            shared.tile([P, T], F32, name="win3", align_bytes=64, offset=1024),
+        ]
+        r = [
+            shared.tile([P, 4, 128], F32, name="r0", align_bytes=64, offset=12288),
+            shared.tile([P, 4, 128], F32, name="r1", align_bytes=64, offset=2048),
+            shared.tile([P, 4, 256], F32, name="r2", align_bytes=64, offset=3072),
+        ]
+        gs = [keep.tile([P, b - a], U8, name=f"gs{u}", align_bytes=64) for u, (a, b) in enumerate(UNITS)]
+        hw = [keep.tile([P, b - a], U32, name=f"hw{u}", align_bytes=64) for u, (a, b) in enumerate(UNITS)]
+        hs = [keep.tile([P, b - a], U8, name=f"hs{u}", align_bytes=64) for u, (a, b) in enumerate(UNITS)]
+        banks = [psum.tile([P, 512], F32, name=f"bank{i}") for i in range(8)]
+        a_parts = (((0, 0, 2), (1, 2, 4)), ((5, 0, 4),), ((6, 0, 2), (5, 2, 4)))
+        y_parts = (((5, 0, 1), (6, 1, 4)), ((0, 0, 1), (1, 1, 3), (7, 3, 4)), ((2, 0, 1), (3, 1, 3), (4, 3, 4)))
+        y_sb = {}
+        for u, (a, b) in enumerate(UNITS):
+            for bank, lo, hi in y_parts[u]:
+                if (u, lo) == (1, 3):
+                    tile = shared.tile([P, 1, b - a], F32, name="y_late", align_bytes=64, offset=4096)
+                else:
+                    tile = keep.tile([P, hi - lo, b - a], F32, name=f"y_sb{u}_{lo}")
+                y_sb[u, lo] = tile
+
+        def part_view(u, part):
+            bank, lo, hi = part
+            w = UNITS[u][1] - UNITS[u][0]
+            return banks[bank][:, 0 : (hi - lo) * w].rearrange("p (t s) -> p t s", s=w)
+
+        def gather_first():
+            for j in range(4):
+                nc.vector.tensor_copy(xg[0][:, :, j], x_raw[j // 2][:, j % 2, :].indirect(offs_t[:, 0 : W0 // 16]))
+
+        def words(tile, dtype):
+            return tile[:].rearrange("p s j -> p (s j)").bitcast(dtype)
+
+        def gather_rest():
+            for i in range(2):
+                nc.vector.tensor_copy(gp[:, i, :], words(pairs[i], U32).indirect(offs_t[:, W0 // 16 : T // 16]))
+
+        def weave(u, copy, dtype):
+            a, b = UNITS[u]
+            copy(
+                words(xg[u], dtype).rearrange("p (s i) -> p s i", i=2),
+                gp[:, :, a - W0 : b - W0].bitcast(dtype).rearrange("p i s -> p s i"),
+            )
+
+        def quantize_x(u):
+            nc.vector.quantize_mx(
+                out=gw[u][:].bitcast(FP8X4), scales=gs[u][:], in_=xg[u][:].rearrange("p s j -> p (s j)")
+            )
 
         def first(u):
-            e, a, b = UNITS[u]
-            n = 512 // (b - a)
-            for t in range(4):
-                nc.tensor.matmul_mx(
-                    out=(a_hi if u == 0 and t >= 2 else a_ps[u][t // n])[:, t % n, :],
-                    lhsT=w1[e][:, 256 * t : 256 * (t + 1)].bitcast(FP4X4),
-                    lhsT_scale=s1[e][:, P * t : P * (t + 1)],
-                    rhs=gw[e][:, a:b].bitcast(FP8X4),
-                    rhs_scale=gs[e][:, a:b],
-                    start=True,
-                    stop=True,
-                )
+            e = UNITS[u][0] // C
+            for part in a_parts[u]:
+                for t in range(part[1], part[2]):
+                    nc.tensor.matmul_mx(
+                        out=part_view(u, part)[:, t - part[1], :],
+                        lhsT=w1[e][:, 256 * t : 256 * (t + 1)].bitcast(FP4X4),
+                        lhsT_scale=s1[e][:, P * t : P * (t + 1)],
+                        rhs=gw[u][:].bitcast(FP8X4),
+                        rhs_scale=gs[u][:],
+                        start=True,
+                        stop=True,
+                    )
 
-        def hidden(u):
-            e, a, b = UNITS[u]
-            n = 512 // (b - a)
-            if u == 0:
-                nc.scalar.activation(r[u][:, 0:2, :], a_ps[u][0][:, 0:2, :], RELU)
-                nc.scalar.activation(r[u][:, 2:4, :], a_hi[:, 2:4, :], RELU)
-            else:
-                for i, bank in enumerate(a_ps[u]):
-                    nc.scalar.activation(r[u][:, i * n : (i + 1) * n, :], bank, RELU)
+        def relu(u):
+            for part in a_parts[u]:
+                nc.scalar.activation(r[u][:, part[1] : part[2], :], part_view(u, part), RELU)
+
+        def square(u):
+            a, b = UNITS[u]
             for c in range(0, b - a, 128):
                 nc.scalar.activation(
-                    h_grp[u][:, c : c + 128, :], r[u][:, :, c : c + 128].rearrange("p t s -> p s t"), SQUARE
+                    h_grp[u][:, c : c + 128, :].rearrange("p (c i) t -> p c t i", i=4),
+                    r[u][:, :, c : c + 128].rearrange("p t (c i) -> p c t i", i=4),
+                    SQUARE,
                 )
+
+        def quantize_h(u):
             nc.vector.quantize_mx(
                 out=hw[u][:].bitcast(FP8X4), scales=hs[u][:], in_=h_grp[u][:].rearrange("p s t -> p (s t)")
             )
 
         def second(u):
-            e, a, b = UNITS[u]
-            n = 512 // (b - a)
-            for i in range(4):
-                nc.tensor.matmul_mx(
-                    out=(y_first if u == 0 and i == 0 else y_ps[u][i // n])[:, i % n, :],
-                    lhsT=w2[:, e, 256 * i : 256 * (i + 1)].bitcast(FP4X4),
-                    lhsT_scale=s2[:, e, P * i : P * (i + 1)],
-                    rhs=hw[u][:].bitcast(FP8X4),
-                    rhs_scale=hs[u][:],
-                    start=True,
-                    stop=True,
-                )
-            if u == 0:
-                nc.scalar.copy(y_sb[u][:, 0, :], y_first[:, 0, :])
-                nc.scalar.copy(y_sb[u][:, 1:4, :], y_ps[u][0][:, 1:4, :])
-            else:
-                for i, bank in enumerate(y_ps[u]):
-                    nc.scalar.copy(y_sb[u][:, i * n : (i + 1) * n, :], bank)
+            e = UNITS[u][0] // C
+            for part in y_parts[u]:
+                for i in range(part[1], part[2]):
+                    nc.tensor.matmul_mx(
+                        out=part_view(u, part)[:, i - part[1], :],
+                        lhsT=w2[:, e, 256 * i : 256 * (i + 1)].bitcast(FP4X4),
+                        lhsT_scale=s2[:, e, P * i : P * (i + 1)],
+                        rhs=hw[u][:].bitcast(FP8X4),
+                        rhs_scale=hs[u][:],
+                        start=True,
+                        stop=True,
+                    )
+
+        def copy_y(u, parts):
+            for part in parts:
+                nc.scalar.copy(y_sb[u, part[1]][:], part_view(u, part))
 
         def scatter(u, i):
-            e, a, b = UNITS[u]
-            nc.vector.tensor_tensor(
-                win[i][:].indirect(dst_t[:, (e * C + a) // 16 : (e * C + b) // 16]),
-                y_sb[u][:, i, :],
-                gate_t[:, e * C + a : e * C + b],
-                MULT,
-            )
-            if u == len(UNITS) - 1:
+            a, b = UNITS[u]
+            lo = max(part[1] for part in y_parts[u] if part[1] <= i)
+            y = y_sb[u, lo][:, i - lo, :]
+            nc.vector.tensor_tensor(win[i][:].indirect(dst_t[:, a // 16 : b // 16]), y, gate_t[:, a:b], MULT)
+            if b == T:
                 nc.sync.dma_start(out[i * P : (i + 1) * P, :], win[i][:])
 
-        gather(0)
-        first(0)
-        hidden(0)
-        gather(1)
-        first(1)
-        second(0)
-        gather(2)
-        w1.append(keep.tile([P, 2 * H], U8, name="w1_1", tag="grp1", align_bytes=64))
-        s1.append(keep.tile([P, H], U8, name="s1_1", tag="slot384", align_bytes=64))
-        permute_words(1, w1[1])
+        pair_up(0)
+        gather_first()
+        quantize_x(0)
         permute_scales(1, s1[1])
-        scatter(0, 0)
-        hidden(1)
-        first(2)
-        hidden(2)
-        for i in range(1, 4):
+        permute_words(1, w1[1])
+        pair_up(1)
+        first(0)
+        relu(0)
+        square(0)
+        gather_rest()
+        quantize_h(0)
+        second(0)
+        weave(1, nc.scalar.copy, U32)
+        weave(2, nc.vector.tensor_copy, I32)
+        copy_y(0, y_parts[0])
+        quantize_x(1)
+        quantize_x(2)
+        first(1)
+        for i in range(3):
             scatter(0, i)
+        relu(1)
+        first(2)
+        square(1)
+        quantize_h(1)
+        relu(2)
         second(1)
-        for i in range(4):
+        copy_y(1, y_parts[1][0:2])
+        scatter(0, 3)
+        square(2)
+        copy_y(1, y_parts[1][2:3])
+        for i in range(3):
             scatter(1, i)
+        quantize_h(2)
         second(2)
+        copy_y(2, y_parts[2])
+        scatter(1, 3)
         for i in range(4):
             scatter(2, i)

@@ -98,41 +98,44 @@ def tile_moe_two_mlp_relu2_kernel(tc, xT, w1_words, w1_scales, w2_words, w2_scal
                 x_raw[i][:].rearrange("p j (c i) -> p c j i", i=4),
             )
 
-        rest = T - W0
         xg = [
             shared.tile([P, 128, 4], BF16, name="xg0", align_bytes=64, offset=16384),
-            shared.tile([P, 128, 4], BF16, name="xg1", align_bytes=64, offset=12864),
-            shared.tile([P, 256, 4], BF16, name="xg2", align_bytes=64, offset=10304),
+            keep.tile([P, 128, 4], BF16, name="xg1", align_bytes=64),
+            shared.tile([P, 256, 4], BF16, name="xg2", align_bytes=64, offset=12288),
         ]
-        gp = shared.tile([P, 2, rest], U32, name="gp", align_bytes=64, offset=16384)
+        gp = shared.tile([P, 2, 256], U32, name="gp", align_bytes=64, offset=16384)
         h_grp = [
             keep.tile([P, 128, 4], BF16, name="h_grp0", align_bytes=64),
-            keep.tile([P, 128, 4], BF16, name="h_grp1", align_bytes=64),
+            shared.tile([P, 128, 4], BF16, name="h_grp1", align_bytes=64, offset=20480),
             keep.tile([P, 256, 4], BF16, name="h_grp2", align_bytes=64),
         ]
         gw = [keep.tile([P, b - a], U32, name=f"gw{u}", align_bytes=64) for u, (a, b) in enumerate(UNITS)]
         win = [
             keep.tile([P, T], F32, name="win0"),
             keep.tile([P, T], F32, name="win1"),
-            keep.tile([P, T], F32, name="win2"),
-            shared.tile([P, T], F32, name="win3", align_bytes=64, offset=1024),
+            shared.tile([P, T], F32, name="win2", align_bytes=64, offset=1024),
+            shared.tile([P, T], F32, name="win3", align_bytes=64, offset=3072),
         ]
         r = [
             shared.tile([P, 4, 128], F32, name="r0", align_bytes=64, offset=12288),
             shared.tile([P, 4, 128], F32, name="r1", align_bytes=64, offset=2048),
-            shared.tile([P, 4, 256], F32, name="r2", align_bytes=64, offset=3072),
+            shared.tile([P, 4, 256], F32, name="r2", align_bytes=64, offset=6144),
         ]
         gs = [keep.tile([P, b - a], U8, name=f"gs{u}", align_bytes=64) for u, (a, b) in enumerate(UNITS)]
-        hw = [keep.tile([P, b - a], U32, name=f"hw{u}", align_bytes=64) for u, (a, b) in enumerate(UNITS)]
+        hw = [
+            shared.tile([P, 128], U32, name="hw0", align_bytes=64, offset=20480),
+            keep.tile([P, 128], U32, name="hw1", align_bytes=64),
+            keep.tile([P, 256], U32, name="hw2", align_bytes=64),
+        ]
         hs = [keep.tile([P, b - a], U8, name=f"hs{u}", align_bytes=64) for u, (a, b) in enumerate(UNITS)]
         banks = [psum.tile([P, 512], F32, name=f"bank{i}") for i in range(8)]
-        a_parts = (((0, 0, 2), (1, 2, 4)), ((5, 0, 4),), ((6, 0, 2), (5, 2, 4)))
-        y_parts = (((5, 0, 1), (6, 1, 4)), ((0, 0, 1), (1, 1, 3), (7, 3, 4)), ((2, 0, 1), (3, 1, 3), (4, 3, 4)))
+        a_parts = (((0, 0, 2), (1, 2, 4)), ((2, 0, 4),), ((5, 0, 2), (6, 2, 4)))
+        y_parts = (((5, 0, 1), (6, 1, 4)), ((0, 0, 1), (1, 1, 2), (7, 2, 4)), ((2, 0, 1), (3, 1, 3), (4, 3, 4)))
         y_sb = {}
         for u, (a, b) in enumerate(UNITS):
             for bank, lo, hi in y_parts[u]:
-                if (u, lo) == (1, 3):
-                    tile = shared.tile([P, 1, b - a], F32, name="y_late", align_bytes=64, offset=4096)
+                if (u, lo) == (1, 2):
+                    tile = shared.tile([P, 2, b - a], F32, name="y_late", align_bytes=64, offset=6144)
                 else:
                     tile = keep.tile([P, hi - lo, b - a], F32, name=f"y_sb{u}_{lo}")
                 y_sb[u, lo] = tile
@@ -149,15 +152,21 @@ def tile_moe_two_mlp_relu2_kernel(tc, xT, w1_words, w1_scales, w2_words, w2_scal
         def words(tile, dtype):
             return tile[:].rearrange("p s j -> p (s j)").bitcast(dtype)
 
-        def gather_rest():
-            for i in range(2):
-                nc.vector.tensor_copy(gp[:, i, :], words(pairs[i], U32).indirect(offs_t[:, W0 // 16 : T // 16]))
-
-        def weave(u, copy, dtype):
+        def gather_pairs(u, i, dest):
             a, b = UNITS[u]
-            copy(
-                words(xg[u], dtype).rearrange("p (s i) -> p s i", i=2),
-                gp[:, :, a - W0 : b - W0].bitcast(dtype).rearrange("p i s -> p s i"),
+            nc.vector.tensor_copy(dest, words(pairs[i], U32).indirect(offs_t[:, a // 16 : b // 16]))
+
+        def gather_second():
+            for i in range(2):
+                gather_pairs(1, i, words(xg[1], U32).rearrange("p (s i) -> p s i", i=2)[:, :, i])
+
+        def gather_third():
+            for i in range(2):
+                gather_pairs(2, i, gp[:, i, :])
+
+        def weave_third():
+            nc.vector.tensor_copy(
+                words(xg[2], I32).rearrange("p (s i) -> p s i", i=2), gp[:].bitcast(I32).rearrange("p i s -> p s i")
             )
 
         def quantize_x(u):
@@ -232,32 +241,34 @@ def tile_moe_two_mlp_relu2_kernel(tc, xT, w1_words, w1_scales, w2_words, w2_scal
         first(0)
         relu(0)
         square(0)
-        gather_rest()
+        gather_second()
+        quantize_x(1)
+        gather_third()
+        first(1)
         quantize_h(0)
         second(0)
-        weave(1, nc.scalar.copy, U32)
-        weave(2, nc.vector.tensor_copy, I32)
-        copy_y(0, y_parts[0])
-        quantize_x(1)
-        quantize_x(2)
-        first(1)
-        for i in range(3):
-            scatter(0, i)
         relu(1)
-        first(2)
+        copy_y(0, y_parts[0])
+        weave_third()
+        quantize_x(2)
+        for i in range(2):
+            scatter(0, i)
         square(1)
+        first(2)
         quantize_h(1)
-        relu(2)
         second(1)
         copy_y(1, y_parts[1][0:2])
-        scatter(0, 3)
+        relu(2)
+        for i in range(2, 4):
+            scatter(0, i)
         square(2)
         copy_y(1, y_parts[1][2:3])
-        for i in range(3):
+        for i in range(2):
             scatter(1, i)
         quantize_h(2)
         second(2)
         copy_y(2, y_parts[2])
-        scatter(1, 3)
+        for i in range(2, 4):
+            scatter(1, i)
         for i in range(4):
             scatter(2, i)

@@ -32,17 +32,15 @@ def tile_moe_two_mlp_relu2_kernel(tc, xT, w1_words, w1_scales, w2_words, w2_scal
         dst_t = keep.tile([P, T // 16], U16, name="dst_t")
         s1_raw = keep.tile([P, E, H], U8, name="s1_raw", align_bytes=64)
         s2 = keep.tile([P, E, N], U8, name="s2", align_bytes=64)
-        warm = keep.tile([P, 1], F32, name="warm")
         w1_raw = keep.tile([P, E, 2 * H], U8, name="w1_raw", align_bytes=64)
         w2 = keep.tile([P, E, 2 * N], U8, name="w2", align_bytes=64)
         x_raw = [
-            keep.tile([P, 2, T], F32, name="x_raw0", align_bytes=64),
-            keep.tile([P, 2, T], F32, name="x_raw1", align_bytes=64),
+            shared.tile([P, 2, T], F32, name="x_raw0", align_bytes=64, offset=28672),
+            shared.tile([P, 2, T], F32, name="x_raw1", align_bytes=64, offset=24576),
         ]
         gate_t = keep.tile([P, E * C], F32, name="gate_t")
 
         nc.gpsimd.memset(s1_raw[:].rearrange("p e i -> p (e i)").bitcast(I32), 0)
-        nc.vector.memset(warm[:], 0.0)
         nc.vector.memset(s2[:].rearrange("p e i -> p (e i)").bitcast(I32), 0)
 
         x_rows = xT.rearrange("(p j) w -> p j w", j=4)
@@ -51,7 +49,6 @@ def tile_moe_two_mlp_relu2_kernel(tc, xT, w1_words, w1_scales, w2_words, w2_scal
                 s1_raw[32 * q : 32 * q + 4].bitcast(I32),
                 w1_scales[:, 0, 4 * q : 4 * q + 4, :].rearrange("e q i -> q e i").bitcast(I32),
             )
-        nc.scalar.activation(warm[:], warm[:], SQUARE)
         nc.sync.dma_start(offs_t[:], offs)
         nc.sync.dma_start(w1_raw[:, 0, :].bitcast(I32), w1_words[0, 0].bitcast(I32))
         nc.sync.dma_start(x_raw[0][:], x_rows[:, 0:2, :])
@@ -81,14 +78,13 @@ def tile_moe_two_mlp_relu2_kernel(tc, xT, w1_words, w1_scales, w2_words, w2_scal
 
         w1 = [
             keep.tile([P, 2 * H], U8, name="w1_0", align_bytes=64),
-            keep.tile([P, 2 * H], U8, name="w1_1", align_bytes=64),
+            shared.tile([P, 2 * H], U8, name="w1_1", align_bytes=64, offset=24576),
         ]
         s1 = [
-            keep.tile([P, H], U8, name="s1_0", align_bytes=64),
-            keep.tile([P, H], U8, name="s1_1", align_bytes=64),
+            shared.tile([P, H], U8, name="s1_0", align_bytes=64, offset=28672),
+            shared.tile([P, H], U8, name="s1_1", align_bytes=64, offset=25600),
         ]
         permute_words(0, w1[0])
-        permute_scales(0, s1[0])
 
         pairs = [keep.tile([P, T, 2], BF16, name=f"pairs{i}", align_bytes=64) for i in range(2)]
 
@@ -128,9 +124,9 @@ def tile_moe_two_mlp_relu2_kernel(tc, xT, w1_words, w1_scales, w2_words, w2_scal
             keep.tile([P, 256], U32, name="hw2", align_bytes=64),
         ]
         hs = [keep.tile([P, b - a], U8, name=f"hs{u}", align_bytes=64) for u, (a, b) in enumerate(UNITS)]
-        banks = [psum.tile([P, 512], F32, name=f"bank{i}") for i in range(8)]
+        banks = [psum.tile([P, 512], F32, name=f"bank{i}") for i in range(7)]
         a_parts = (((0, 0, 2), (1, 2, 4)), ((2, 0, 4),), ((5, 0, 2), (6, 2, 4)))
-        y_parts = (((5, 0, 1), (6, 1, 4)), ((0, 0, 1), (1, 1, 2), (7, 2, 4)), ((2, 0, 1), (3, 1, 3), (4, 3, 4)))
+        y_parts = (((5, 0, 1), (6, 1, 4)), ((0, 0, 2), (1, 2, 4)), ((2, 0, 1), (3, 1, 3), (4, 3, 4)))
         y_sb = {}
         for u, (a, b) in enumerate(UNITS):
             for bank, lo, hi in y_parts[u]:
@@ -234,9 +230,8 @@ def tile_moe_two_mlp_relu2_kernel(tc, xT, w1_words, w1_scales, w2_words, w2_scal
 
         pair_up(0)
         gather_first()
+        permute_scales(0, s1[0])
         quantize_x(0)
-        permute_scales(1, s1[1])
-        permute_words(1, w1[1])
         pair_up(1)
         first(0)
         relu(0)
@@ -244,6 +239,8 @@ def tile_moe_two_mlp_relu2_kernel(tc, xT, w1_words, w1_scales, w2_words, w2_scal
         gather_second()
         quantize_x(1)
         gather_third()
+        permute_words(1, w1[1])
+        permute_scales(1, s1[1])
         first(1)
         quantize_h(0)
         second(0)
@@ -257,12 +254,12 @@ def tile_moe_two_mlp_relu2_kernel(tc, xT, w1_words, w1_scales, w2_words, w2_scal
         first(2)
         quantize_h(1)
         second(1)
-        copy_y(1, y_parts[1][0:2])
+        copy_y(1, y_parts[1][0:1])
         relu(2)
         for i in range(2, 4):
             scatter(0, i)
         square(2)
-        copy_y(1, y_parts[1][2:3])
+        copy_y(1, y_parts[1][1:2])
         for i in range(2):
             scatter(1, i)
         quantize_h(2)

@@ -96,7 +96,7 @@ def tile_moe_two_mlp_relu2_kernel(tc, xT, w1_words, w1_scales, w2_words, w2_scal
 
         xg = [
             shared.tile([P, 128, 4], BF16, name="xg0", align_bytes=64, offset=16384),
-            keep.tile([P, 128, 4], BF16, name="xg1", align_bytes=64),
+            shared.tile([P, 128, 4], BF16, name="xg1", align_bytes=64, offset=17408),
             shared.tile([P, 256, 4], BF16, name="xg2", align_bytes=64, offset=12288),
         ]
         gp = shared.tile([P, 2, 256], U32, name="gp", align_bytes=64, offset=16384)

@@ -1,6 +1,7 @@
 from contextlib import ExitStack
 
 import concourse.mybir as mybir
+from concourse.masks import make_identity
 
 F32 = mybir.dt.float32
 BF16 = mybir.dt.bfloat16
@@ -41,6 +42,7 @@ def tile_moe_two_mlp_relu2_kernel(tc, xT, w1_words, w1_scales, w2_words, w2_scal
         gate_t = keep.tile([P, E * C], F32, name="gate_t")
 
         nc.gpsimd.memset(s1_raw[:].rearrange("p e i -> p (e i)").bitcast(I32), 0)
+        ident = keep.tile([P, P], F32, name="ident")
         nc.vector.memset(s2[:].rearrange("p e i -> p (e i)").bitcast(I32), 0)
 
         x_rows = xT.rearrange("(p j) w -> p j w", j=4)
@@ -64,6 +66,8 @@ def tile_moe_two_mlp_relu2_kernel(tc, xT, w1_words, w1_scales, w2_words, w2_scal
         nc.sync.dma_start(gate_t[:], gate[0:P, :])
         nc.sync.dma_start(dst_t[:], dst)
 
+        make_identity(nc, ident[:])
+
         def permute_words(e, dest):
             nc.vector.tensor_copy(
                 dest[:].bitcast(U16).rearrange("p (t m) -> p t m", t=4),
@@ -78,11 +82,9 @@ def tile_moe_two_mlp_relu2_kernel(tc, xT, w1_words, w1_scales, w2_words, w2_scal
 
         w1 = [
             keep.tile([P, 2 * H], U8, name="w1_0", align_bytes=64),
-            shared.tile([P, 2 * H], U8, name="w1_1", align_bytes=64, offset=24576),
         ]
         s1 = [
             shared.tile([P, H], U8, name="s1_0", align_bytes=64, offset=28672),
-            shared.tile([P, H], U8, name="s1_1", align_bytes=64, offset=25600),
         ]
         permute_words(0, w1[0])
 
@@ -115,7 +117,7 @@ def tile_moe_two_mlp_relu2_kernel(tc, xT, w1_words, w1_scales, w2_words, w2_scal
         r = [
             shared.tile([P, 4, 128], F32, name="r0", align_bytes=64, offset=12288),
             shared.tile([P, 4, 128], F32, name="r1", align_bytes=64, offset=2048),
-            shared.tile([P, 4, 256], F32, name="r2", align_bytes=64, offset=6144),
+            shared.tile([P, 2, 4, 128], F32, name="r2", align_bytes=64, offset=6144),
         ]
         gs = [keep.tile([P, b - a], U8, name=f"gs{u}", align_bytes=64) for u, (a, b) in enumerate(UNITS)]
         hw = [
@@ -197,6 +199,32 @@ def tile_moe_two_mlp_relu2_kernel(tc, xT, w1_words, w1_scales, w2_words, w2_scal
                     SQUARE,
                 )
 
+        def first_turned():
+            for c in range(2):
+                nc.tensor.matmul_mx(
+                    out=banks[5 + c][:],
+                    lhsT=gw[2][:, P * c : P * (c + 1)].bitcast(FP8X4),
+                    lhsT_scale=gs[2][:, P * c : P * (c + 1)],
+                    rhs=w1_raw[:, 1, :].bitcast(FP4X4),
+                    rhs_scale=s1_raw[:, 1, :],
+                    start=True,
+                    stop=True,
+                )
+
+        def relu_turned():
+            for c in range(2):
+                nc.scalar.activation(r[2][:, c, :, :], banks[5 + c][:].rearrange("s (m t) -> s t m", t=4), RELU)
+                for t in range(4):
+                    nc.tensor.transpose(banks[3 + c][:, P * t : P * (t + 1)], r[2][:, c, t, :], ident[:])
+
+        def square_turned():
+            for c in range(2):
+                nc.scalar.activation(
+                    h_grp[2][:, P * c : P * (c + 1), :].rearrange("p (c i) t -> p c t i", i=4),
+                    banks[3 + c][:].rearrange("p (t c i) -> p c t i", t=4, i=4),
+                    SQUARE,
+                )
+
         def quantize_h(u):
             nc.vector.quantize_mx(
                 out=hw[u][:].bitcast(FP8X4), scales=hs[u][:], in_=h_grp[u][:].rearrange("p s t -> p (s t)")
@@ -239,8 +267,6 @@ def tile_moe_two_mlp_relu2_kernel(tc, xT, w1_words, w1_scales, w2_words, w2_scal
         gather_second()
         quantize_x(1)
         gather_third()
-        permute_words(1, w1[1])
-        permute_scales(1, s1[1])
         first(1)
         quantize_h(0)
         second(0)
@@ -251,14 +277,14 @@ def tile_moe_two_mlp_relu2_kernel(tc, xT, w1_words, w1_scales, w2_words, w2_scal
         for i in range(2):
             scatter(0, i)
         square(1)
-        first(2)
+        first_turned()
         quantize_h(1)
         second(1)
         copy_y(1, y_parts[1][0:1])
-        relu(2)
+        relu_turned()
         for i in range(2, 4):
             scatter(0, i)
-        square(2)
+        square_turned()
         copy_y(1, y_parts[1][1:2])
         for i in range(2):
             scatter(1, i)

@@ -17,8 +17,7 @@ SQUARE = mybir.ActivationFunctionType.Square
 
 P = 128
 K, T, E, C, H, N = 512, 512, 2, 256, 512, 512
-UNITS = ((0, 128), (128, 256), (256, 512))
-W0 = 128
+GROUPS = ((0, 64), (64, 128), (128, 256), (256, 384), (384, 512))
 FLOPS = 2 * E * C * H * (K + N)
 
 
@@ -29,6 +28,7 @@ def tile_moe_two_mlp_relu2_kernel(tc, xT, w1_words, w1_scales, w2_words, w2_scal
         shared = ctx.enter_context(tc.tile_pool(name="shared", bufs=1))
         psum = ctx.enter_context(tc.psum_pool(name="psum", bufs=1))
 
+        width = [b - a for a, b in GROUPS]
         offs_t = keep.tile([P, T // 16], U16, name="offs_t")
         dst_t = keep.tile([P, T // 16], U16, name="dst_t")
         s1_raw = keep.tile([P, E, H], U8, name="s1_raw", align_bytes=64)
@@ -36,59 +36,98 @@ def tile_moe_two_mlp_relu2_kernel(tc, xT, w1_words, w1_scales, w2_words, w2_scal
         w1_raw = keep.tile([P, E, 2 * H], U8, name="w1_raw", align_bytes=64)
         w2 = keep.tile([P, E, 2 * N], U8, name="w2", align_bytes=64)
         x_raw = [
-            shared.tile([P, 2, T], F32, name="x_raw0", align_bytes=64, offset=28672),
-            shared.tile([P, 2, T], F32, name="x_raw1", align_bytes=64, offset=24576),
+            keep.tile([P, 2, T], F32, name="x_raw0", align_bytes=64),
+            keep.tile([P, 2, T], F32, name="x_raw1", align_bytes=64),
         ]
         gate_t = keep.tile([P, E * C], F32, name="gate_t")
-
-        nc.gpsimd.memset(s1_raw[:].rearrange("p e i -> p (e i)").bitcast(I32), 0)
         ident = keep.tile([P, P], F32, name="ident")
-        nc.vector.memset(s2[:].rearrange("p e i -> p (e i)").bitcast(I32), 0)
+
+        nc.gpsimd.memset(s1_raw[:, 0, :].bitcast(I32), 0)
 
         x_rows = xT.rearrange("(p j) w -> p j w", j=4)
-        for q in range(4):
-            (nc.scalar if q < 3 else nc.gpsimd).dma_start(
+
+        def load_s1(queue, q):
+            queue.dma_start(
                 s1_raw[32 * q : 32 * q + 4].bitcast(I32),
                 w1_scales[:, 0, 4 * q : 4 * q + 4, :].rearrange("e q i -> q e i").bitcast(I32),
             )
+
+        for q in range(3):
+            load_s1(nc.scalar, q)
         nc.sync.dma_start(offs_t[:], offs)
         nc.sync.dma_start(w1_raw[:, 0, :].bitcast(I32), w1_words[0, 0].bitcast(I32))
         nc.sync.dma_start(x_raw[0][:], x_rows[:, 0:2, :])
         nc.sync.dma_start(x_raw[1][:, 0, :], x_rows[:, 2, :])
         nc.sync.dma_start(x_raw[1][:, 1, :], x_rows[:, 3, :])
-        nc.sync.dma_start(w1_raw[:, 1, :].bitcast(I32), w1_words[1, 0].bitcast(I32))
+        load_s1(nc.sync, 3)
         nc.sync.dma_start(w2[:].bitcast(I32), w2_words[:, 0].rearrange("e p b -> p e b").bitcast(I32))
         for q in range(4):
             nc.sync.dma_start(
                 s2[32 * q : 32 * q + 4].bitcast(I32),
                 w2_scales[:, 0, 4 * q : 4 * q + 4, :].rearrange("e q i -> q e i").bitcast(I32),
             )
-        nc.sync.dma_start(gate_t[:], gate[0:P, :])
         nc.sync.dma_start(dst_t[:], dst)
+        nc.sync.dma_start(gate_t[:], gate[0:P, :])
+        nc.sync.dma_start(w1_raw[:, 1, :].bitcast(I32), w1_words[1, 0].bitcast(I32))
 
         make_identity(nc, ident[:])
 
-        def permute_words(e, dest):
-            nc.vector.tensor_copy(
-                dest[:].bitcast(U16).rearrange("p (t m) -> p t m", t=4),
-                w1_raw[:, e, :].bitcast(U16).rearrange("p (m t) -> p t m", t=4),
-            )
-
-        def permute_scales(e, dest):
-            nc.vector.tensor_copy(
-                dest[:].rearrange("p (t m) -> p t m", t=4),
-                s1_raw[:, e, :].rearrange("p (m t) -> p t m", t=4),
-            )
-
-        w1 = [
-            keep.tile([P, 2 * H], U8, name="w1_0", align_bytes=64),
-        ]
-        s1 = [
-            shared.tile([P, H], U8, name="s1_0", align_bytes=64, offset=28672),
-        ]
-        permute_words(0, w1[0])
-
+        w1 = keep.tile([P, 2 * H], U8, name="w1", align_bytes=64)
+        s1 = keep.tile([P, H], U8, name="s1", align_bytes=64)
         pairs = [keep.tile([P, T, 2], BF16, name=f"pairs{i}", align_bytes=64) for i in range(2)]
+        xg = [keep.tile([P, width[g], 4], BF16, name=f"xg{g}", align_bytes=64) for g in range(5)]
+        r = [
+            shared.tile([P, 4, 64], F32, name="r0", align_bytes=64, offset=4096),
+            keep.tile([P, 4, 64], F32, name="r1", align_bytes=64),
+            keep.tile([P, 4, P], F32, name="r2", align_bytes=64),
+            shared.tile([P, 4, P], F32, name="r3", align_bytes=64, offset=8192),
+            shared.tile([P, 4, P], F32, name="r4", align_bytes=64, offset=12288),
+        ]
+        gp = {
+            3: keep.tile([P, 2, P], U32, name="gp3", align_bytes=64),
+            4: shared.tile([P, 2, P], U32, name="gp4", align_bytes=64, offset=4096),
+        }
+        hg = [keep.tile([P, width[g], 4], BF16, name=f"hg{g}", align_bytes=64) for g in range(5)]
+        xw = [keep.tile([P, P], U32, name=f"xw{g}", align_bytes=64) for g in range(5)]
+        xs = [keep.tile([P, P], U8, name=f"xs{g}", align_bytes=64) for g in range(5)]
+        hw = [keep.tile([P, P], U32, name=f"hw{g}", align_bytes=64) for g in range(5)]
+        hs = [keep.tile([P, P], U8, name=f"hs{g}", align_bytes=64) for g in range(5)]
+        win = [keep.tile([P, T], F32, name=f"win{i}") for i in range(4)]
+        banks = [psum.tile([P, 4, P], F32, name=f"bank{i}") for i in range(8)]
+        a_parts = (((0, 0, 2), (1, 2, 4)), ((0, 0, 4),), ((1, 0, 2), (0, 2, 4)))
+        y_parts = (
+            ((2, 0, 1), (3, 1, 4)),
+            ((4, 0, 4),),
+            ((2, 0, 2), (1, 2, 4)),
+            ((4, 0, 2), (7, 2, 4)),
+            ((5, 0, 1), (0, 1, 4)),
+        )
+        a_bank = {3: 3, 4: 3}
+        t_bank = {3: 5, 4: 6}
+        y_sb = {}
+        for g in range(5):
+            for bank, lo, hi in y_parts[g]:
+                if (g, lo) in ((2, 2), (3, 2)):
+                    y_sb[g, lo] = shared.tile([P, 2, P], F32, name=f"y_late{g}", align_bytes=64, offset=4096 * g)
+                else:
+                    y_sb[g, lo] = keep.tile([P, hi - lo, width[g]], F32, name=f"y_sb{g}_{lo}")
+
+        for g in range(2):
+            for codes, scales in ((xw[g], xs[g]), (hw[g], hs[g])):
+                nc.vector.memset(codes[:, 64:P].bitcast(I32), 0)
+                nc.vector.memset(scales[:, 64:P].bitcast(I32), 0)
+
+        def permute_words():
+            nc.vector.tensor_copy(
+                w1[:].bitcast(U16).rearrange("p (t m) -> p t m", t=4),
+                w1_raw[:, 0, :].bitcast(U16).rearrange("p (m t) -> p t m", t=4),
+            )
+
+        def permute_scales():
+            nc.vector.tensor_copy(
+                s1[:].rearrange("p (t m) -> p t m", t=4),
+                s1_raw[:, 0, :].rearrange("p (m t) -> p t m", t=4),
+            )
 
         def pair_up(i):
             nc.scalar.copy(
@@ -96,202 +135,159 @@ def tile_moe_two_mlp_relu2_kernel(tc, xT, w1_words, w1_scales, w2_words, w2_scal
                 x_raw[i][:].rearrange("p j (c i) -> p c j i", i=4),
             )
 
-        xg = [
-            shared.tile([P, 128, 4], BF16, name="xg0", align_bytes=64, offset=16384),
-            shared.tile([P, 128, 4], BF16, name="xg1", align_bytes=64, offset=17408),
-            shared.tile([P, 256, 4], BF16, name="xg2", align_bytes=64, offset=12288),
-        ]
-        gp = shared.tile([P, 2, 256], U32, name="gp", align_bytes=64, offset=16384)
-        h_grp = [
-            keep.tile([P, 128, 4], BF16, name="h_grp0", align_bytes=64),
-            shared.tile([P, 128, 4], BF16, name="h_grp1", align_bytes=64, offset=20480),
-            keep.tile([P, 256, 4], BF16, name="h_grp2", align_bytes=64),
-        ]
-        gw = [keep.tile([P, b - a], U32, name=f"gw{u}", align_bytes=64) for u, (a, b) in enumerate(UNITS)]
-        win = [
-            keep.tile([P, T], F32, name="win0"),
-            keep.tile([P, T], F32, name="win1"),
-            shared.tile([P, T], F32, name="win2", align_bytes=64, offset=1024),
-            shared.tile([P, T], F32, name="win3", align_bytes=64, offset=3072),
-        ]
-        r = [
-            shared.tile([P, 4, 128], F32, name="r0", align_bytes=64, offset=12288),
-            shared.tile([P, 4, 128], F32, name="r1", align_bytes=64, offset=2048),
-            shared.tile([P, 2, 4, 128], F32, name="r2", align_bytes=64, offset=6144),
-        ]
-        gs = [keep.tile([P, b - a], U8, name=f"gs{u}", align_bytes=64) for u, (a, b) in enumerate(UNITS)]
-        hw = [
-            shared.tile([P, 128], U32, name="hw0", align_bytes=64, offset=20480),
-            keep.tile([P, 128], U32, name="hw1", align_bytes=64),
-            keep.tile([P, 256], U32, name="hw2", align_bytes=64),
-        ]
-        hs = [keep.tile([P, b - a], U8, name=f"hs{u}", align_bytes=64) for u, (a, b) in enumerate(UNITS)]
-        banks = [psum.tile([P, 512], F32, name=f"bank{i}") for i in range(7)]
-        a_parts = (((0, 0, 2), (1, 2, 4)), ((2, 0, 4),), ((5, 0, 2), (6, 2, 4)))
-        y_parts = (((5, 0, 1), (6, 1, 4)), ((0, 0, 2), (1, 2, 4)), ((2, 0, 1), (3, 1, 3), (4, 3, 4)))
-        y_sb = {}
-        for u, (a, b) in enumerate(UNITS):
-            for bank, lo, hi in y_parts[u]:
-                if (u, lo) == (1, 2):
-                    tile = shared.tile([P, 2, b - a], F32, name="y_late", align_bytes=64, offset=6144)
-                else:
-                    tile = keep.tile([P, hi - lo, b - a], F32, name=f"y_sb{u}_{lo}")
-                y_sb[u, lo] = tile
-
-        def part_view(u, part):
-            bank, lo, hi = part
-            w = UNITS[u][1] - UNITS[u][0]
-            return banks[bank][:, 0 : (hi - lo) * w].rearrange("p (t s) -> p t s", s=w)
-
-        def gather_first():
-            for j in range(4):
-                nc.vector.tensor_copy(xg[0][:, :, j], x_raw[j // 2][:, j % 2, :].indirect(offs_t[:, 0 : W0 // 16]))
-
         def words(tile, dtype):
             return tile[:].rearrange("p s j -> p (s j)").bitcast(dtype)
 
-        def gather_pairs(u, i, dest):
-            a, b = UNITS[u]
-            nc.vector.tensor_copy(dest, words(pairs[i], U32).indirect(offs_t[:, a // 16 : b // 16]))
+        def tokens(g):
+            a, b = GROUPS[g]
+            return offs_t[:, a // 16 : b // 16]
 
-        def gather_second():
-            for i in range(2):
-                gather_pairs(1, i, words(xg[1], U32).rearrange("p (s i) -> p s i", i=2)[:, :, i])
+        def gather_plane(g, j):
+            nc.vector.tensor_copy(xg[g][:, :, j], x_raw[j // 2][:, j % 2, :].indirect(tokens(g)))
 
-        def gather_third():
-            for i in range(2):
-                gather_pairs(2, i, gp[:, i, :])
+        def gather_pair(g, i):
+            if g < 3:
+                dest = words(xg[g], U32).rearrange("p (s i) -> p s i", i=2)[:, :, i]
+            else:
+                dest = gp[g][:, i, :]
+            nc.vector.tensor_copy(dest, words(pairs[i], U32).indirect(tokens(g)))
 
-        def weave_third():
+        def weave(g):
             nc.vector.tensor_copy(
-                words(xg[2], I32).rearrange("p (s i) -> p s i", i=2), gp[:].bitcast(I32).rearrange("p i s -> p s i")
+                words(xg[g], I32).rearrange("p (s i) -> p s i", i=2), gp[g][:].bitcast(I32).rearrange("p i s -> p s i")
             )
 
-        def quantize_x(u):
+        def quantize(codes, scales, values, g):
             nc.vector.quantize_mx(
-                out=gw[u][:].bitcast(FP8X4), scales=gs[u][:], in_=xg[u][:].rearrange("p s j -> p (s j)")
+                out=codes[g][:, 0 : width[g]].bitcast(FP8X4),
+                scales=scales[g][:, 0 : width[g]],
+                in_=values[g][:].rearrange("p s j -> p (s j)"),
             )
 
-        def first(u):
-            e = UNITS[u][0] // C
-            for part in a_parts[u]:
-                for t in range(part[1], part[2]):
-                    nc.tensor.matmul_mx(
-                        out=part_view(u, part)[:, t - part[1], :],
-                        lhsT=w1[e][:, 256 * t : 256 * (t + 1)].bitcast(FP4X4),
-                        lhsT_scale=s1[e][:, P * t : P * (t + 1)],
-                        rhs=gw[u][:].bitcast(FP8X4),
-                        rhs_scale=gs[u][:],
-                        start=True,
-                        stop=True,
-                    )
-
-        def relu(u):
-            for part in a_parts[u]:
-                nc.scalar.activation(r[u][:, part[1] : part[2], :], part_view(u, part), RELU)
-
-        def square(u):
-            a, b = UNITS[u]
-            for c in range(0, b - a, 128):
-                nc.scalar.activation(
-                    h_grp[u][:, c : c + 128, :].rearrange("p (c i) t -> p c t i", i=4),
-                    r[u][:, :, c : c + 128].rearrange("p t (c i) -> p c t i", i=4),
-                    SQUARE,
-                )
-
-        def first_turned():
-            for c in range(2):
+        def product(part, weights, weight_scales, codes, scales):
+            bank, lo, hi = part
+            for t in range(lo, hi):
                 nc.tensor.matmul_mx(
-                    out=banks[5 + c][:],
-                    lhsT=gw[2][:, P * c : P * (c + 1)].bitcast(FP8X4),
-                    lhsT_scale=gs[2][:, P * c : P * (c + 1)],
-                    rhs=w1_raw[:, 1, :].bitcast(FP4X4),
-                    rhs_scale=s1_raw[:, 1, :],
+                    out=banks[bank][:, t - lo, :],
+                    lhsT=weights[:, 256 * t : 256 * (t + 1)].bitcast(FP4X4),
+                    lhsT_scale=weight_scales[:, P * t : P * (t + 1)],
+                    rhs=codes[:].bitcast(FP8X4),
+                    rhs_scale=scales[:],
                     start=True,
                     stop=True,
                 )
 
-        def relu_turned():
-            for c in range(2):
-                nc.scalar.activation(r[2][:, c, :, :], banks[5 + c][:].rearrange("s (m t) -> s t m", t=4), RELU)
-                for t in range(4):
-                    nc.tensor.transpose(banks[3 + c][:, P * t : P * (t + 1)], r[2][:, c, t, :], ident[:])
+        def first(g, k):
+            product(a_parts[g][k], w1, s1, xw[g], xs[g])
 
-        def square_turned():
-            for c in range(2):
-                nc.scalar.activation(
-                    h_grp[2][:, P * c : P * (c + 1), :].rearrange("p (c i) t -> p c t i", i=4),
-                    banks[3 + c][:].rearrange("p (t c i) -> p c t i", t=4, i=4),
-                    SQUARE,
-                )
+        def second(g):
+            e = GROUPS[g][0] // C
+            for part in y_parts[g]:
+                product(part, w2[:, e, :], s2[:, e, :], hw[g], hs[g])
 
-        def quantize_h(u):
-            nc.vector.quantize_mx(
-                out=hw[u][:].bitcast(FP8X4), scales=hs[u][:], in_=h_grp[u][:].rearrange("p s t -> p (s t)")
+        def relu(g, k):
+            bank, lo, hi = a_parts[g][k]
+            nc.scalar.activation(r[g][:, lo:hi, :], banks[bank][:, 0 : hi - lo, 0 : width[g]], RELU)
+
+        def square(g, source):
+            nc.scalar.activation(
+                hg[g][:].rearrange("p (c i) t -> p c t i", i=4),
+                source[:].rearrange("p t (c i) -> p c t i", i=4),
+                SQUARE,
             )
 
-        def second(u):
-            e = UNITS[u][0] // C
-            for part in y_parts[u]:
-                for i in range(part[1], part[2]):
-                    nc.tensor.matmul_mx(
-                        out=part_view(u, part)[:, i - part[1], :],
-                        lhsT=w2[:, e, 256 * i : 256 * (i + 1)].bitcast(FP4X4),
-                        lhsT_scale=s2[:, e, P * i : P * (i + 1)],
-                        rhs=hw[u][:].bitcast(FP8X4),
-                        rhs_scale=hs[u][:],
-                        start=True,
-                        stop=True,
-                    )
+        def first_turned(g):
+            nc.tensor.matmul_mx(
+                out=banks[a_bank[g]][:].rearrange("s t m -> s (t m)"),
+                lhsT=xw[g][:].bitcast(FP8X4),
+                lhsT_scale=xs[g][:],
+                rhs=w1_raw[:, 1, :].bitcast(FP4X4),
+                rhs_scale=s1_raw[:, 1, :],
+                start=True,
+                stop=True,
+            )
 
-        def copy_y(u, parts):
-            for part in parts:
-                nc.scalar.copy(y_sb[u, part[1]][:], part_view(u, part))
+        def relu_turned(g):
+            nc.scalar.activation(
+                r[g][:], banks[a_bank[g]][:].rearrange("s a b -> s (a b)").rearrange("s (m t) -> s t m", t=4), RELU
+            )
+            for t in range(4):
+                nc.tensor.transpose(banks[t_bank[g]][:, t, :], r[g][:, t, :], ident[:])
 
-        def scatter(u, i):
-            a, b = UNITS[u]
-            lo = max(part[1] for part in y_parts[u] if part[1] <= i)
-            y = y_sb[u, lo][:, i - lo, :]
-            nc.vector.tensor_tensor(win[i][:].indirect(dst_t[:, a // 16 : b // 16]), y, gate_t[:, a:b], MULT)
-            if b == T:
-                nc.sync.dma_start(out[i * P : (i + 1) * P, :], win[i][:])
+        def copy_y(g, k):
+            bank, lo, hi = y_parts[g][k]
+            nc.scalar.copy(y_sb[g, lo][:], banks[bank][:, 0 : hi - lo, 0 : width[g]])
+
+        def scatter(g, blocks):
+            a, b = GROUPS[g]
+            for i in blocks:
+                lo = max(part[1] for part in y_parts[g] if part[1] <= i)
+                y = y_sb[g, lo][:, i - lo, :]
+                nc.vector.tensor_tensor(win[i][:].indirect(dst_t[:, a // 16 : b // 16]), y, gate_t[:, a:b], MULT)
+                if b == T:
+                    nc.sync.dma_start(out[i * P : (i + 1) * P, :], win[i][:])
 
         pair_up(0)
-        gather_first()
-        permute_scales(0, s1[0])
-        quantize_x(0)
+        for j in range(4):
+            gather_plane(0, j)
+        permute_words()
+        permute_scales()
+        quantize(xw, xs, xg, 0)
         pair_up(1)
-        first(0)
-        relu(0)
-        square(0)
-        gather_second()
-        quantize_x(1)
-        gather_third()
-        first(1)
-        quantize_h(0)
+        first(0, 0)
+        first(0, 1)
+        relu(0, 0)
+        relu(0, 1)
+        square(0, r[0])
+        quantize(hw, hs, hg, 0)
+        gather_pair(1, 0)
+        gather_plane(1, 2)
+        gather_plane(1, 3)
+        quantize(xw, xs, xg, 1)
+        first(1, 0)
+        relu(1, 0)
+        gather_pair(2, 0)
+        gather_pair(2, 1)
+        quantize(xw, xs, xg, 2)
         second(0)
-        relu(1)
-        copy_y(0, y_parts[0])
-        weave_third()
-        quantize_x(2)
-        for i in range(2):
-            scatter(0, i)
-        square(1)
-        first_turned()
-        quantize_h(1)
+        first(2, 0)
+        square(1, r[1])
+        quantize(hw, hs, hg, 1)
+        copy_y(0, 0)
+        copy_y(0, 1)
+        relu(2, 0)
+        first(2, 1)
+        relu(2, 1)
         second(1)
-        copy_y(1, y_parts[1][0:1])
-        relu_turned()
-        for i in range(2, 4):
-            scatter(0, i)
-        square_turned()
-        copy_y(1, y_parts[1][1:2])
-        for i in range(2):
-            scatter(1, i)
-        quantize_h(2)
+        for g in (3, 4):
+            gather_pair(g, 0)
+            gather_pair(g, 1)
+            weave(g)
+            quantize(xw, xs, xg, g)
+        square(2, r[2])
+        copy_y(1, 0)
+        scatter(0, range(4))
+        quantize(hw, hs, hg, 2)
         second(2)
-        copy_y(2, y_parts[2])
-        for i in range(2, 4):
-            scatter(1, i)
-        for i in range(4):
-            scatter(2, i)
+        first_turned(3)
+        copy_y(2, 0)
+        relu_turned(3)
+        scatter(1, range(4))
+        scatter(2, range(2))
+        square(3, banks[t_bank[3]])
+        copy_y(2, 1)
+        quantize(hw, hs, hg, 3)
+        second(3)
+        first_turned(4)
+        copy_y(3, 0)
+        relu_turned(4)
+        scatter(2, range(2, 4))
+        scatter(3, range(2))
+        square(4, banks[t_bank[4]])
+        copy_y(3, 1)
+        quantize(hw, hs, hg, 4)
+        second(4)
+        copy_y(4, 0)
+        copy_y(4, 1)
+        scatter(3, range(2, 4))
+        scatter(4, range(4))

@@ -54,8 +54,8 @@ def tile_moe_two_mlp_relu2_kernel(tc, xT, w1_words, w1_scales, w2_words, w2_scal
 
         for q in range(3):
             load_s1(nc.scalar, q)
-        nc.sync.dma_start(offs_t[:], offs)
         nc.sync.dma_start(w1_raw[:, 0, :].bitcast(I32), w1_words[0, 0].bitcast(I32))
+        nc.sync.dma_start(offs_t[:], offs)
         nc.sync.dma_start(x_raw[0][:], x_rows[:, 0:2, :])
         nc.sync.dma_start(x_raw[1][:, 0, :], x_rows[:, 2, :])
         nc.sync.dma_start(x_raw[1][:, 1, :], x_rows[:, 3, :])
@@ -75,11 +75,12 @@ def tile_moe_two_mlp_relu2_kernel(tc, xT, w1_words, w1_scales, w2_words, w2_scal
         w1 = keep.tile([P, 2 * H], U8, name="w1", align_bytes=64)
         s1 = keep.tile([P, H], U8, name="s1", align_bytes=64)
         pairs = [keep.tile([P, T, 2], BF16, name=f"pairs{i}", align_bytes=64) for i in range(2)]
-        xg = [keep.tile([P, width[g], 4], BF16, name=f"xg{g}", align_bytes=64) for g in range(5)]
+        xg = [keep.tile([P, width[g], 4], BF16, name=f"xg{g}", align_bytes=64) for g in range(4)]
+        xg.append(shared.tile([P, P, 4], BF16, name="xg4", align_bytes=64, offset=16384))
         r = [
             shared.tile([P, 4, 64], F32, name="r0", align_bytes=64, offset=4096),
             keep.tile([P, 4, 64], F32, name="r1", align_bytes=64),
-            keep.tile([P, 4, P], F32, name="r2", align_bytes=64),
+            shared.tile([P, 4, P], F32, name="r2", align_bytes=64, offset=16384),
             shared.tile([P, 4, P], F32, name="r3", align_bytes=64, offset=8192),
             shared.tile([P, 4, P], F32, name="r4", align_bytes=64, offset=12288),
         ]
@@ -94,7 +95,7 @@ def tile_moe_two_mlp_relu2_kernel(tc, xT, w1_words, w1_scales, w2_words, w2_scal
         hs = [keep.tile([P, P], U8, name=f"hs{g}", align_bytes=64) for g in range(5)]
         win = [keep.tile([P, T], F32, name=f"win{i}") for i in range(4)]
         banks = [psum.tile([P, 4, P], F32, name=f"bank{i}") for i in range(8)]
-        a_parts = (((0, 0, 2), (1, 2, 4)), ((0, 0, 4),), ((1, 0, 2), (0, 2, 4)))
+        a_parts = (((0, 0, 2), (1, 2, 3), (7, 3, 4)), ((0, 0, 4),), ((1, 0, 2), (0, 2, 4)))
         y_parts = (
             ((2, 0, 1), (3, 1, 4)),
             ((4, 0, 4),),
@@ -153,9 +154,13 @@ def tile_moe_two_mlp_relu2_kernel(tc, xT, w1_words, w1_scales, w2_words, w2_scal
             nc.vector.tensor_copy(dest, words(pairs[i], U32).indirect(tokens(g)))
 
         def weave(g):
-            nc.vector.tensor_copy(
-                words(xg[g], I32).rearrange("p (s i) -> p s i", i=2), gp[g][:].bitcast(I32).rearrange("p i s -> p s i")
-            )
+            if g == 3:
+                nc.vector.tensor_copy(
+                    words(xg[g], I32).rearrange("p (s i) -> p s i", i=2),
+                    gp[g][:].bitcast(I32).rearrange("p i s -> p s i"),
+                )
+            else:
+                nc.scalar.copy(words(xg[g], U32).rearrange("p (s i) -> p s i", i=2), gp[g][:].rearrange("p i s -> p s i"))
 
         def quantize(codes, scales, values, g):
             nc.vector.quantize_mx(
@@ -234,10 +239,10 @@ def tile_moe_two_mlp_relu2_kernel(tc, xT, w1_words, w1_scales, w2_words, w2_scal
         permute_scales()
         quantize(xw, xs, xg, 0)
         pair_up(1)
-        first(0, 0)
-        first(0, 1)
-        relu(0, 0)
-        relu(0, 1)
+        for k in range(3):
+            first(0, k)
+        for k in range(3):
+            relu(0, k)
         square(0, r[0])
         quantize(hw, hs, hg, 0)
         gather_pair(1, 0)
@@ -262,12 +267,15 @@ def tile_moe_two_mlp_relu2_kernel(tc, xT, w1_words, w1_scales, w2_words, w2_scal
         for g in (3, 4):
             gather_pair(g, 0)
             gather_pair(g, 1)
-            weave(g)
-            quantize(xw, xs, xg, g)
+            if g == 3:
+                weave(g)
+                quantize(xw, xs, xg, g)
         square(2, r[2])
         copy_y(1, 0)
+        weave(4)
         scatter(0, range(4))
         quantize(hw, hs, hg, 2)
+        quantize(xw, xs, xg, 4)
         second(2)
         first_turned(3)
         copy_y(2, 0)

@@ -1,7 +1,6 @@
 from contextlib import ExitStack
 
 import concourse.mybir as mybir
-from concourse.masks import make_identity
 
 F32 = mybir.dt.float32
 BF16 = mybir.dt.bfloat16
@@ -12,12 +11,12 @@ U8 = mybir.dt.uint8
 FP8X4 = mybir.dt.float8_e4m3fn_x4
 FP4X4 = mybir.dt.float4_e2m1fn_x4
 MULT = mybir.AluOpType.mult
+COPY = mybir.ActivationFunctionType.Copy
 RELU = mybir.ActivationFunctionType.Relu
 SQUARE = mybir.ActivationFunctionType.Square
 
 P = 128
 K, T, E, C, H, N = 512, 512, 2, 256, 512, 512
-GROUPS = ((0, 64), (64, 128), (128, 256), (256, 384), (384, 512))
 FLOPS = 2 * E * C * H * (K + N)
 
 
@@ -28,274 +27,185 @@ def tile_moe_two_mlp_relu2_kernel(tc, xT, w1_words, w1_scales, w2_words, w2_scal
         shared = ctx.enter_context(tc.tile_pool(name="shared", bufs=1))
         psum = ctx.enter_context(tc.psum_pool(name="psum", bufs=1))
 
-        width = [b - a for a, b in GROUPS]
         offs_t = keep.tile([P, T // 16], U16, name="offs_t")
         dst_t = keep.tile([P, T // 16], U16, name="dst_t")
         s1_raw = keep.tile([P, E, H], U8, name="s1_raw", align_bytes=64)
         s2 = keep.tile([P, E, N], U8, name="s2", align_bytes=64)
-        w1_raw = keep.tile([P, E, 2 * H], U8, name="w1_raw", align_bytes=64)
+        w1_raw = [keep.tile([P, 2 * H], U8, name=f"w1_raw{e}", align_bytes=64) for e in range(E)]
         w2 = keep.tile([P, E, 2 * N], U8, name="w2", align_bytes=64)
-        x_raw = [
-            keep.tile([P, 2, T], F32, name="x_raw0", align_bytes=64),
-            keep.tile([P, 2, T], F32, name="x_raw1", align_bytes=64),
-        ]
+        planes = [keep.tile([P, T], F32, name=f"plane{j}", align_bytes=64) for j in range(4)]
         gate_t = keep.tile([P, E * C], F32, name="gate_t")
-        ident = keep.tile([P, P], F32, name="ident")
 
-        nc.gpsimd.memset(s1_raw[:, 0, :].bitcast(I32), 0)
+        nc.gpsimd.memset(s1_raw[:].rearrange("p e i -> p (e i)").bitcast(I32), 0)
+
+        def load_scales(queue, tile, scales, q):
+            queue.dma_start(
+                tile[32 * q : 32 * q + 4].bitcast(I32),
+                scales[:, 0, 4 * q : 4 * q + 4, :].rearrange("e q i -> q e i").bitcast(I32),
+            )
 
         x_rows = xT.rearrange("(p j) w -> p j w", j=4)
-
-        def load_s1(queue, q):
-            queue.dma_start(
-                s1_raw[32 * q : 32 * q + 4].bitcast(I32),
-                w1_scales[:, 0, 4 * q : 4 * q + 4, :].rearrange("e q i -> q e i").bitcast(I32),
-            )
-
-        for q in range(3):
-            load_s1(nc.scalar, q)
-        nc.sync.dma_start(w1_raw[:, 0, :].bitcast(I32), w1_words[0, 0].bitcast(I32))
+        for q in range(2):
+            load_scales(nc.scalar, s1_raw, w1_scales, q)
+        nc.sync.dma_start(w1_raw[0][:].bitcast(I32), w1_words[0, 0].bitcast(I32))
         nc.sync.dma_start(offs_t[:], offs)
-        nc.sync.dma_start(x_raw[0][:], x_rows[:, 0:2, :])
-        nc.sync.dma_start(x_raw[1][:, 0, :], x_rows[:, 2, :])
-        nc.sync.dma_start(x_raw[1][:, 1, :], x_rows[:, 3, :])
-        load_s1(nc.sync, 3)
+        for j in range(4):
+            nc.sync.dma_start(planes[j][:], x_rows[:, j, :])
+        for q in range(2, 4):
+            load_scales(nc.sync, s1_raw, w1_scales, q)
+        nc.sync.dma_start(w1_raw[1][:].bitcast(I32), w1_words[1, 0].bitcast(I32))
         nc.sync.dma_start(w2[:].bitcast(I32), w2_words[:, 0].rearrange("e p b -> p e b").bitcast(I32))
         for q in range(4):
-            nc.sync.dma_start(
-                s2[32 * q : 32 * q + 4].bitcast(I32),
-                w2_scales[:, 0, 4 * q : 4 * q + 4, :].rearrange("e q i -> q e i").bitcast(I32),
-            )
-        nc.sync.dma_start(dst_t[:], dst)
+            load_scales(nc.sync, s2, w2_scales, q)
         nc.sync.dma_start(gate_t[:], gate[0:P, :])
-        nc.sync.dma_start(w1_raw[:, 1, :].bitcast(I32), w1_words[1, 0].bitcast(I32))
+        nc.sync.dma_start(dst_t[:], dst)
 
-        make_identity(nc, ident[:])
-
-        w1 = keep.tile([P, 2 * H], U8, name="w1", align_bytes=64)
-        s1 = keep.tile([P, H], U8, name="s1", align_bytes=64)
-        pairs = [keep.tile([P, T, 2], BF16, name=f"pairs{i}", align_bytes=64) for i in range(2)]
-        xg = [keep.tile([P, width[g], 4], BF16, name=f"xg{g}", align_bytes=64) for g in range(4)]
-        xg.append(shared.tile([P, P, 4], BF16, name="xg4", align_bytes=64, offset=16384))
-        r = [
-            shared.tile([P, 4, 64], F32, name="r0", align_bytes=64, offset=4096),
-            keep.tile([P, 4, 64], F32, name="r1", align_bytes=64),
-            shared.tile([P, 4, P], F32, name="r2", align_bytes=64, offset=16384),
-            shared.tile([P, 4, P], F32, name="r3", align_bytes=64, offset=8192),
-            shared.tile([P, 4, P], F32, name="r4", align_bytes=64, offset=12288),
+        w1 = [keep.tile([P, 2 * H], U8, name=f"w1_{e}", align_bytes=64) for e in range(E)]
+        s1 = [
+            keep.tile([P, H], U8, name="s1_0", align_bytes=64),
+            shared.tile([P, H], U8, name="s1_1", align_bytes=64, offset=1024),
         ]
-        gp = {
-            3: keep.tile([P, 2, P], U32, name="gp3", align_bytes=64),
-            4: shared.tile([P, 2, P], U32, name="gp4", align_bytes=64, offset=4096),
-        }
-        hg = [keep.tile([P, width[g], 4], BF16, name=f"hg{g}", align_bytes=64) for g in range(5)]
-        xw = [keep.tile([P, P], U32, name=f"xw{g}", align_bytes=64) for g in range(5)]
-        xs = [keep.tile([P, P], U8, name=f"xs{g}", align_bytes=64) for g in range(5)]
-        hw = [keep.tile([P, P], U32, name=f"hw{g}", align_bytes=64) for g in range(5)]
-        hs = [keep.tile([P, P], U8, name=f"hs{g}", align_bytes=64) for g in range(5)]
-        win = [keep.tile([P, T], F32, name=f"win{i}") for i in range(4)]
-        banks = [psum.tile([P, 4, P], F32, name=f"bank{i}") for i in range(8)]
-        a_parts = (((0, 0, 2), (1, 2, 3), (7, 3, 4)), ((0, 0, 4),), ((1, 0, 2), (0, 2, 4)))
-        y_parts = (
-            ((2, 0, 1), (3, 1, 4)),
-            ((4, 0, 4),),
-            ((2, 0, 2), (1, 2, 4)),
-            ((4, 0, 2), (7, 2, 4)),
-            ((5, 0, 1), (0, 1, 4)),
-        )
-        a_bank = {3: 3, 4: 3}
-        t_bank = {3: 5, 4: 6}
-        y_sb = {}
-        for g in range(5):
-            for bank, lo, hi in y_parts[g]:
-                if (g, lo) in ((2, 2), (3, 2)):
-                    y_sb[g, lo] = shared.tile([P, 2, P], F32, name=f"y_late{g}", align_bytes=64, offset=4096 * g)
-                else:
-                    y_sb[g, lo] = keep.tile([P, hi - lo, width[g]], F32, name=f"y_sb{g}_{lo}")
+        picked = [keep.tile([P, 4, C], BF16, name=f"picked{e}", align_bytes=64) for e in range(E)]
+        xg = [shared.tile([P, P, 4], BF16, name=f"xg{g}", align_bytes=64, offset=1024 * (g % 3)) for g in range(4)]
+        xw = [keep.tile([P, P], U32, name=f"xw{g}", align_bytes=64) for g in range(4)]
+        xs = [keep.tile([P, P], U8, name=f"xs{g}", align_bytes=64) for g in range(4)]
+        r = [keep.tile([P, 4 * P], F32, name=f"r{g}", align_bytes=64) for g in range(4)]
+        hg = [keep.tile([P, 4 * P], BF16, name=f"hg{g}", align_bytes=64) for g in range(2)]
+        hg_late = shared.tile([P, 2, 4 * P], BF16, name="hg_late", align_bytes=64, offset=4096)
+        hw = [keep.tile([P, w], U32, name=f"hw{u}", align_bytes=64) for u, w in enumerate((P, P, C))]
+        hs = [keep.tile([P, w], U8, name=f"hs{u}", align_bytes=64) for u, w in enumerate((P, P, C))]
+        y = [keep.tile([P, 4, P], F32, name=f"y{u}", align_bytes=64) for u in range(2)]
+        y_late = [keep.tile([P, 2, C], F32, name=f"y_late{half}", align_bytes=64) for half in range(2)]
+        win = [keep.tile([P, T], F32, name=f"win{i}") for i in (0, 2, 3)]
+        win.insert(1, shared.tile([P, T], F32, name="win1", align_bytes=64, offset=4096))
+        banks = [psum.tile([P, 4 * P], F32, name=f"bank{i}") for i in range(8)]
+        units = ((0, P), (P, C), (C, T))
 
-        for g in range(2):
-            for codes, scales in ((xw[g], xs[g]), (hw[g], hs[g])):
-                nc.vector.memset(codes[:, 64:P].bitcast(I32), 0)
-                nc.vector.memset(scales[:, 64:P].bitcast(I32), 0)
-
-        def permute_words():
-            nc.vector.tensor_copy(
-                w1[:].bitcast(U16).rearrange("p (t m) -> p t m", t=4),
-                w1_raw[:, 0, :].bitcast(U16).rearrange("p (m t) -> p t m", t=4),
-            )
-
-        def permute_scales():
-            nc.vector.tensor_copy(
-                s1[:].rearrange("p (t m) -> p t m", t=4),
-                s1_raw[:, 0, :].rearrange("p (m t) -> p t m", t=4),
-            )
-
-        def pair_up(i):
+        def permute_words(e):
             nc.scalar.copy(
-                pairs[i][:].rearrange("p (c i) j -> p c j i", i=4),
-                x_raw[i][:].rearrange("p j (c i) -> p c j i", i=4),
+                w1[e][:].bitcast(U16).rearrange("p (t m) -> p t m", t=4),
+                w1_raw[e][:].bitcast(U16).rearrange("p (m t) -> p t m", t=4),
             )
 
-        def words(tile, dtype):
-            return tile[:].rearrange("p s j -> p (s j)").bitcast(dtype)
+        def permute_scales(e):
+            nc.vector.tensor_copy(
+                s1[e][:].rearrange("p (t m) -> p t m", t=4),
+                s1_raw[:, e, :].rearrange("p (m t) -> p t m", t=4),
+            )
 
-        def tokens(g):
-            a, b = GROUPS[g]
-            return offs_t[:, a // 16 : b // 16]
-
-        def gather_plane(g, j):
-            nc.vector.tensor_copy(xg[g][:, :, j], x_raw[j // 2][:, j % 2, :].indirect(tokens(g)))
-
-        def gather_pair(g, i):
-            if g < 3:
-                dest = words(xg[g], U32).rearrange("p (s i) -> p s i", i=2)[:, :, i]
+        def gather(j, a, b, on_vector):
+            dest = picked[a // C][:, j, a % C : a % C + b - a]
+            source = planes[j][:].indirect(offs_t[:, a // 16 : b // 16])
+            if on_vector:
+                nc.vector.tensor_copy(dest, source)
             else:
-                dest = gp[g][:, i, :]
-            nc.vector.tensor_copy(dest, words(pairs[i], U32).indirect(tokens(g)))
+                nc.scalar.activation(dest, source, COPY)
 
-        def weave(g):
-            if g == 3:
-                nc.vector.tensor_copy(
-                    words(xg[g], I32).rearrange("p (s i) -> p s i", i=2),
-                    gp[g][:].bitcast(I32).rearrange("p i s -> p s i"),
-                )
-            else:
-                nc.scalar.copy(words(xg[g], U32).rearrange("p (s i) -> p s i", i=2), gp[g][:].rearrange("p i s -> p s i"))
-
-        def quantize(codes, scales, values, g):
-            nc.vector.quantize_mx(
-                out=codes[g][:, 0 : width[g]].bitcast(FP8X4),
-                scales=scales[g][:, 0 : width[g]],
-                in_=values[g][:].rearrange("p s j -> p (s j)"),
+        def interleave(g):
+            copy = nc.vector.tensor_copy if g in (0, 3) else nc.scalar.copy
+            copy(
+                xg[g][:].rearrange("p (c i) j -> p c j i", i=4),
+                picked[g // 2][:, :, P * (g % 2) : P * (g % 2 + 1)].rearrange("p j (c i) -> p c j i", i=4),
             )
 
-        def product(part, weights, weight_scales, codes, scales):
-            bank, lo, hi = part
-            for t in range(lo, hi):
-                nc.tensor.matmul_mx(
-                    out=banks[bank][:, t - lo, :],
-                    lhsT=weights[:, 256 * t : 256 * (t + 1)].bitcast(FP4X4),
-                    lhsT_scale=weight_scales[:, P * t : P * (t + 1)],
-                    rhs=codes[:].bitcast(FP8X4),
-                    rhs_scale=scales[:],
-                    start=True,
-                    stop=True,
-                )
+        def quantize(codes, scales, values):
+            nc.vector.quantize_mx(out=codes.bitcast(FP8X4), scales=scales, in_=values)
 
-        def first(g, k):
-            product(a_parts[g][k], w1, s1, xw[g], xs[g])
-
-        def second(g):
-            e = GROUPS[g][0] // C
-            for part in y_parts[g]:
-                product(part, w2[:, e, :], s2[:, e, :], hw[g], hs[g])
-
-        def relu(g, k):
-            bank, lo, hi = a_parts[g][k]
-            nc.scalar.activation(r[g][:, lo:hi, :], banks[bank][:, 0 : hi - lo, 0 : width[g]], RELU)
-
-        def square(g, source):
-            nc.scalar.activation(
-                hg[g][:].rearrange("p (c i) t -> p c t i", i=4),
-                source[:].rearrange("p t (c i) -> p c t i", i=4),
-                SQUARE,
-            )
-
-        def first_turned(g):
+        def product(dest, weights, weight_scales, block, codes, scales):
             nc.tensor.matmul_mx(
-                out=banks[a_bank[g]][:].rearrange("s t m -> s (t m)"),
-                lhsT=xw[g][:].bitcast(FP8X4),
-                lhsT_scale=xs[g][:],
-                rhs=w1_raw[:, 1, :].bitcast(FP4X4),
-                rhs_scale=s1_raw[:, 1, :],
+                out=dest,
+                lhsT=weights[:, 256 * block : 256 * (block + 1)].bitcast(FP4X4),
+                lhsT_scale=weight_scales[:, P * block : P * (block + 1)],
+                rhs=codes[:].bitcast(FP8X4),
+                rhs_scale=scales[:],
                 start=True,
                 stop=True,
             )
 
-        def relu_turned(g):
-            nc.scalar.activation(
-                r[g][:], banks[a_bank[g]][:].rearrange("s a b -> s (a b)").rearrange("s (m t) -> s t m", t=4), RELU
-            )
+        def first(g):
+            quantize(xw[g][:], xs[g][:], xg[g][:].rearrange("p s j -> p (s j)"))
             for t in range(4):
-                nc.tensor.transpose(banks[t_bank[g]][:, t, :], r[g][:, t, :], ident[:])
+                product(banks[g][:, P * t : P * (t + 1)], w1[g // 2], s1[g // 2], t, xw[g], xs[g])
 
-        def copy_y(g, k):
-            bank, lo, hi = y_parts[g][k]
-            nc.scalar.copy(y_sb[g, lo][:], banks[bank][:, 0 : hi - lo, 0 : width[g]])
+        def woven(g):
+            return banks[g][:].rearrange("p (t s) -> p s t", t=4)
 
-        def scatter(g, blocks):
-            a, b = GROUPS[g]
-            for i in blocks:
-                lo = max(part[1] for part in y_parts[g] if part[1] <= i)
-                y = y_sb[g, lo][:, i - lo, :]
-                nc.vector.tensor_tensor(win[i][:].indirect(dst_t[:, a // 16 : b // 16]), y, gate_t[:, a:b], MULT)
-                if b == T:
-                    nc.sync.dma_start(out[i * P : (i + 1) * P, :], win[i][:])
+        def rows(g):
+            return r[g][:].rearrange("p (s t) -> p s t", t=4)
 
-        pair_up(0)
-        for j in range(4):
-            gather_plane(0, j)
-        permute_words()
-        permute_scales()
-        quantize(xw, xs, xg, 0)
-        pair_up(1)
-        for k in range(3):
-            first(0, k)
-        for k in range(3):
-            relu(0, k)
-        square(0, r[0])
-        quantize(hw, hs, hg, 0)
-        gather_pair(1, 0)
-        gather_plane(1, 2)
-        gather_plane(1, 3)
-        quantize(xw, xs, xg, 1)
-        first(1, 0)
-        relu(1, 0)
-        gather_pair(2, 0)
-        gather_pair(2, 1)
-        quantize(xw, xs, xg, 2)
-        second(0)
-        first(2, 0)
-        square(1, r[1])
-        quantize(hw, hs, hg, 1)
-        copy_y(0, 0)
-        copy_y(0, 1)
-        relu(2, 0)
-        first(2, 1)
-        relu(2, 1)
-        second(1)
-        for g in (3, 4):
-            gather_pair(g, 0)
-            gather_pair(g, 1)
-            if g == 3:
-                weave(g)
-                quantize(xw, xs, xg, g)
-        square(2, r[2])
-        copy_y(1, 0)
-        weave(4)
-        scatter(0, range(4))
-        quantize(hw, hs, hg, 2)
-        quantize(xw, xs, xg, 4)
-        second(2)
-        first_turned(3)
-        copy_y(2, 0)
-        relu_turned(3)
-        scatter(1, range(4))
-        scatter(2, range(2))
-        square(3, banks[t_bank[3]])
-        copy_y(2, 1)
-        quantize(hw, hs, hg, 3)
-        second(3)
-        first_turned(4)
-        copy_y(3, 0)
-        relu_turned(4)
-        scatter(2, range(2, 4))
-        scatter(3, range(2))
-        square(4, banks[t_bank[4]])
-        copy_y(3, 1)
-        quantize(hw, hs, hg, 4)
-        second(4)
-        copy_y(4, 0)
-        copy_y(4, 1)
-        scatter(3, range(2, 4))
-        scatter(4, range(4))
+        def second(u, blocks, bank):
+            a, b = units[u]
+            e = a // C
+            for k, block in enumerate(blocks):
+                product(banks[bank][:, k * (b - a) : (k + 1) * (b - a)], w2[:, e, :], s2[:, e, :], block, hw[u], hs[u])
+
+        def gated(dest, u, bank):
+            a, b = units[u]
+            count = 4 * P // (b - a)
+            nc.vector.tensor_tensor(
+                dest[:],
+                banks[bank][:].rearrange("p (k s) -> p k s", k=count),
+                gate_t[:, a:b].unsqueeze(1).to_broadcast([P, count, b - a]),
+                MULT,
+            )
+
+        def scatter(u, i):
+            a, b = units[u]
+            places = win[i][:].indirect(dst_t[:, a // 16 : b // 16])
+            values = y[u][:, i, :] if u < 2 else y_late[i // 2][:, i % 2, :]
+            if i >= 2:
+                nc.scalar.activation(places, values, COPY)
+            elif u == 2:
+                nc.vector.tensor_tensor(places, values, gate_t[:, a:b], MULT)
+            else:
+                nc.vector.tensor_copy(places, values)
+            if u == 2:
+                nc.sync.dma_start(out[i * P : (i + 1) * P, :], win[i][:])
+
+        permute_words(0)
+        for j in range(3):
+            gather(j, 0, C, True)
+            gather(j, C, T, False)
+        gather(3, 0, P, True)
+        gather(3, P, C, False)
+        gather(3, C, T, False)
+        permute_scales(0)
+        interleave(0)
+        first(0)
+        interleave(1)
+        interleave(2)
+        first(1)
+        interleave(3)
+        permute_words(1)
+        permute_scales(1)
+        first(2)
+        first(3)
+
+        for half in range(2):
+            nc.scalar.activation(rows(0)[:, 64 * half : 64 * (half + 1), :], woven(0)[:, 64 * half : 64 * (half + 1), :], RELU)
+        for half in range(2):
+            nc.scalar.activation(hg[0][:, C * half : C * (half + 1)], r[0][:, C * half : C * (half + 1)], SQUARE)
+        nc.vector.tensor_scalar_max(rows(1), woven(1), 0.0)
+        quantize(hw[0][:], hs[0][:], hg[0][:])
+        second(0, range(4), 4)
+        nc.scalar.activation(hg[1][:], r[1][:], SQUARE)
+        nc.vector.tensor_scalar_max(rows(2), woven(2), 0.0)
+        nc.scalar.activation(rows(3), woven(3), RELU)
+        for g in range(2, 4):
+            nc.scalar.activation(hg_late[:, g - 2, :], r[g][:], SQUARE)
+        quantize(hw[1][:], hs[1][:], hg[1][:])
+        second(1, range(4), 5)
+        gated(y[0], 0, 4)
+        scatter(0, 0)
+        quantize(hw[2][:], hs[2][:], hg_late[:].rearrange("p g x -> p (g x)"))
+        second(2, range(2), 6)
+        second(2, range(2, 4), 7)
+        gated(y[1], 1, 5)
+        scatter(0, 2)
+        scatter(0, 3)
+        scatter(0, 1)
+        nc.scalar.copy(y_late[0][:].rearrange("p k s -> p (k s)"), banks[6][:])
+        gated(y_late[1], 2, 7)
+        for u in range(1, 3):
+            for i in (2, 0, 3, 1):
+                scatter(u, i)

@@ -29,7 +29,7 @@ def tile_moe_two_mlp_relu2_kernel(tc, xT, w1_words, w1_scales, w2_words, w2_scal
 
         offs_t = keep.tile([P, T // 16], U16, name="offs_t")
         dst_t = keep.tile([P, T // 16], U16, name="dst_t")
-        s1_raw = keep.tile([P, E, H], U8, name="s1_raw", align_bytes=64)
+        s1_raw = shared.tile([P, E, H], U8, name="s1_raw", align_bytes=64, offset=12288)
         s2 = keep.tile([P, E, N], U8, name="s2", align_bytes=64)
         w1_raw = [keep.tile([P, 2 * H], U8, name=f"w1_raw{e}", align_bytes=64) for e in range(E)]
         w2 = keep.tile([P, E, 2 * N], U8, name="w2", align_bytes=64)
@@ -60,17 +60,17 @@ def tile_moe_two_mlp_relu2_kernel(tc, xT, w1_words, w1_scales, w2_words, w2_scal
         nc.sync.dma_start(gate_t[:], gate[0:P, :])
         nc.sync.dma_start(dst_t[:], dst)
 
-        w1 = [keep.tile([P, 2 * H], U8, name=f"w1_{e}", align_bytes=64) for e in range(E)]
-        s1 = [
-            keep.tile([P, H], U8, name="s1_0", align_bytes=64),
-            shared.tile([P, H], U8, name="s1_1", align_bytes=64, offset=1024),
+        w1 = [
+            keep.tile([P, 2 * H], U8, name="w1_0", align_bytes=64),
+            shared.tile([P, 2 * H], U8, name="w1_1", align_bytes=64, offset=12288 + 512),
         ]
+        s1 = [keep.tile([P, H], U8, name=f"s1_{e}", align_bytes=64) for e in range(E)]
         picked = [keep.tile([P, 4, C], BF16, name=f"picked{e}", align_bytes=64) for e in range(E)]
-        xg = [shared.tile([P, P, 4], BF16, name=f"xg{g}", align_bytes=64, offset=1024 * (g % 3)) for g in range(4)]
+        xg = [shared.tile([P, P, 4], BF16, name=f"xg{g}", align_bytes=64, offset=at) for g, at in enumerate((2048, 0, 1024, 12288 - 960))]
         xw = [keep.tile([P, P], U32, name=f"xw{g}", align_bytes=64) for g in range(4)]
-        xs = [keep.tile([P, P], U8, name=f"xs{g}", align_bytes=64) for g in range(4)]
+        xs = [shared.tile([P, P], U8, name=f"xs{g}", align_bytes=64, offset=at) for g, at in enumerate((3072, 12352, 12480, 12608))]
         r = [keep.tile([P, 4 * P], F32, name=f"r{g}", align_bytes=64) for g in range(4)]
-        hg = [keep.tile([P, 4 * P], BF16, name=f"hg{g}", align_bytes=64) for g in range(2)]
+        hg = [shared.tile([P, 4 * P], BF16, name=f"hg{g}", align_bytes=64, offset=8192 + 1024 * g) for g in range(2)]
         hg_late = shared.tile([P, 2, 4 * P], BF16, name="hg_late", align_bytes=64, offset=4096)
         hw = [keep.tile([P, w], U32, name=f"hw{u}", align_bytes=64) for u, w in enumerate((P, P, C))]
         hs = [keep.tile([P, w], U8, name=f"hs{u}", align_bytes=64) for u, w in enumerate((P, P, C))]
@@ -81,10 +81,10 @@ def tile_moe_two_mlp_relu2_kernel(tc, xT, w1_words, w1_scales, w2_words, w2_scal
         banks = [psum.tile([P, 4 * P], F32, name=f"bank{i}") for i in range(8)]
         units = ((0, P), (P, C), (C, T))
 
-        def permute_words(e):
-            nc.scalar.copy(
-                w1[e][:].bitcast(U16).rearrange("p (t m) -> p t m", t=4),
-                w1_raw[e][:].bitcast(U16).rearrange("p (m t) -> p t m", t=4),
+        def permute_words(e, copy, a, b):
+            copy(
+                w1[e][:].bitcast(U16).rearrange("p (t m) -> p t m", t=4)[:, a:b, :],
+                w1_raw[e][:].bitcast(U16).rearrange("p (m t) -> p t m", t=4)[:, a:b, :],
             )
 
         def permute_scales(e):
@@ -101,11 +101,11 @@ def tile_moe_two_mlp_relu2_kernel(tc, xT, w1_words, w1_scales, w2_words, w2_scal
             else:
                 nc.scalar.activation(dest, source, COPY)
 
-        def interleave(g):
-            copy = nc.vector.tensor_copy if g in (0, 3) else nc.scalar.copy
+        def interleave(g, count=4):
+            copy = nc.scalar.copy if g in (1, 2) else nc.vector.tensor_copy
             copy(
-                xg[g][:].rearrange("p (c i) j -> p c j i", i=4),
-                picked[g // 2][:, :, P * (g % 2) : P * (g % 2 + 1)].rearrange("p j (c i) -> p c j i", i=4),
+                xg[g][:, :, 0:count].rearrange("p (c i) j -> p c j i", i=4),
+                picked[g // 2][:, 0:count, P * (g % 2) : P * (g % 2 + 1)].rearrange("p j (c i) -> p c j i", i=4),
             )
 
         def quantize(codes, scales, values):
@@ -162,22 +162,26 @@ def tile_moe_two_mlp_relu2_kernel(tc, xT, w1_words, w1_scales, w2_words, w2_scal
             if u == 2:
                 nc.sync.dma_start(out[i * P : (i + 1) * P, :], win[i][:])
 
-        permute_words(0)
-        for j in range(3):
+        permute_words(0, nc.scalar.copy, 0, 2)
+        permute_words(0, nc.vector.tensor_copy, 2, 4)
+        for j in range(2):
             gather(j, 0, C, True)
             gather(j, C, T, False)
-        gather(3, 0, P, True)
+        gather(2, 0, P, True)
+        gather(2, P, C, False)
+        gather(2, C, T, False)
+        interleave(0, 3)
+        nc.vector.tensor_copy(xg[0][:, :, 3], planes[3][:].indirect(offs_t[:, 0 : P // 16]))
         gather(3, P, C, False)
         gather(3, C, T, False)
         permute_scales(0)
-        interleave(0)
         first(0)
+        permute_scales(1)
         interleave(1)
         interleave(2)
         first(1)
+        permute_words(1, nc.vector.tensor_copy, 0, 4)
         interleave(3)
-        permute_words(1)
-        permute_scales(1)
         first(2)
         first(3)
 
@@ -188,9 +192,9 @@ def tile_moe_two_mlp_relu2_kernel(tc, xT, w1_words, w1_scales, w2_words, w2_scal
         nc.vector.tensor_scalar_max(rows(1), woven(1), 0.0)
         quantize(hw[0][:], hs[0][:], hg[0][:])
         second(0, range(4), 4)
+        nc.scalar.activation(rows(2), woven(2), RELU)
         nc.scalar.activation(hg[1][:], r[1][:], SQUARE)
-        nc.vector.tensor_scalar_max(rows(2), woven(2), 0.0)
-        nc.scalar.activation(rows(3), woven(3), RELU)
+        nc.vector.tensor_scalar_max(rows(3), woven(3), 0.0)
         for g in range(2, 4):
             nc.scalar.activation(hg_late[:, g - 2, :], r[g][:], SQUARE)
         quantize(hw[1][:], hs[1][:], hg[1][:])

@@ -29,7 +29,7 @@ def tile_moe_two_mlp_relu2_kernel(tc, xT, w1_words, w1_scales, w2_words, w2_scal
 
         offs_t = keep.tile([P, T // 16], U16, name="offs_t")
         dst_t = keep.tile([P, T // 16], U16, name="dst_t")
-        s1_raw = shared.tile([P, E, H], U8, name="s1_raw", align_bytes=64, offset=12288)
+        s1_raw = keep.tile([P, E, H], U8, name="s1_raw", align_bytes=64)
         s2 = keep.tile([P, E, N], U8, name="s2", align_bytes=64)
         w1_raw = [keep.tile([P, 2 * H], U8, name=f"w1_raw{e}", align_bytes=64) for e in range(E)]
         w2 = keep.tile([P, E, 2 * N], U8, name="w2", align_bytes=64)
@@ -60,24 +60,25 @@ def tile_moe_two_mlp_relu2_kernel(tc, xT, w1_words, w1_scales, w2_words, w2_scal
         nc.sync.dma_start(gate_t[:], gate[0:P, :])
         nc.sync.dma_start(dst_t[:], dst)
 
-        w1 = [
-            keep.tile([P, 2 * H], U8, name="w1_0", align_bytes=64),
-            shared.tile([P, 2 * H], U8, name="w1_1", align_bytes=64, offset=12288 + 512),
-        ]
+        w1 = [keep.tile([P, 2 * H], U8, name=f"w1_{e}", align_bytes=64) for e in range(E)]
         s1 = [keep.tile([P, H], U8, name=f"s1_{e}", align_bytes=64) for e in range(E)]
         picked = [keep.tile([P, 4, C], BF16, name=f"picked{e}", align_bytes=64) for e in range(E)]
-        xg = [shared.tile([P, P, 4], BF16, name=f"xg{g}", align_bytes=64, offset=at) for g, at in enumerate((2048, 0, 1024, 12288 - 960))]
+        xg = [shared.tile([P, P, 4], BF16, name=f"xg{g}", align_bytes=64, offset=at) for g, at in enumerate((2048, 12288 - 64, 1024, 12288 - 64))]
         xw = [keep.tile([P, P], U32, name=f"xw{g}", align_bytes=64) for g in range(4)]
-        xs = [shared.tile([P, P], U8, name=f"xs{g}", align_bytes=64, offset=at) for g, at in enumerate((3072, 12352, 12480, 12608))]
-        r = [keep.tile([P, 4 * P], F32, name=f"r{g}", align_bytes=64) for g in range(4)]
+        xs_first = keep.tile([P, P], U8, name="xs_first", align_bytes=64)
+        xs = [xs_first[:]] + [s1_raw[:, 0, P * g : P * (g + 1)] for g in range(3)]
+        r = [keep.tile([P, 4 * P], F32, name=f"r{g}", align_bytes=64) for g in (0, 2, 3)]
+        r.insert(1, shared.tile([P, 4 * P], F32, name="r1", align_bytes=64, offset=10240))
         hg = [shared.tile([P, 4 * P], BF16, name=f"hg{g}", align_bytes=64, offset=8192 + 1024 * g) for g in range(2)]
         hg_late = shared.tile([P, 2, 4 * P], BF16, name="hg_late", align_bytes=64, offset=4096)
-        hw = [keep.tile([P, w], U32, name=f"hw{u}", align_bytes=64) for u, w in enumerate((P, P, C))]
+        hw = [keep.tile([P, P], U32, name=f"hw{u}", align_bytes=64) for u in range(2)]
+        hw.append(shared.tile([P, C], U32, name="hw2", align_bytes=64, offset=6144))
         hs = [keep.tile([P, w], U8, name=f"hs{u}", align_bytes=64) for u, w in enumerate((P, P, C))]
-        y = [keep.tile([P, 4, P], F32, name=f"y{u}", align_bytes=64) for u in range(2)]
+        y_early = keep.tile([P, 4, C], F32, name="y_early", align_bytes=64)
+        y = [y_early[:, :, P * u : P * (u + 1)] for u in range(2)]
         y_late = [keep.tile([P, 2, C], F32, name=f"y_late{half}", align_bytes=64) for half in range(2)]
         win = [keep.tile([P, T], F32, name=f"win{i}") for i in (0, 2, 3)]
-        win.insert(1, shared.tile([P, T], F32, name="win1", align_bytes=64, offset=4096))
+        win.insert(1, shared.tile([P, T], F32, name="win1", align_bytes=64, offset=6144))
         banks = [psum.tile([P, 4 * P], F32, name=f"bank{i}") for i in range(8)]
         units = ((0, P), (P, C), (C, T))
 
@@ -117,13 +118,13 @@ def tile_moe_two_mlp_relu2_kernel(tc, xT, w1_words, w1_scales, w2_words, w2_scal
                 lhsT=weights[:, 256 * block : 256 * (block + 1)].bitcast(FP4X4),
                 lhsT_scale=weight_scales[:, P * block : P * (block + 1)],
                 rhs=codes[:].bitcast(FP8X4),
-                rhs_scale=scales[:],
+                rhs_scale=scales,
                 start=True,
                 stop=True,
             )
 
         def first(g):
-            quantize(xw[g][:], xs[g][:], xg[g][:].rearrange("p s j -> p (s j)"))
+            quantize(xw[g][:], xs[g], xg[g][:].rearrange("p s j -> p (s j)"))
             for t in range(4):
                 product(banks[g][:, P * t : P * (t + 1)], w1[g // 2], s1[g // 2], t, xw[g], xs[g])
 
@@ -137,13 +138,13 @@ def tile_moe_two_mlp_relu2_kernel(tc, xT, w1_words, w1_scales, w2_words, w2_scal
             a, b = units[u]
             e = a // C
             for k, block in enumerate(blocks):
-                product(banks[bank][:, k * (b - a) : (k + 1) * (b - a)], w2[:, e, :], s2[:, e, :], block, hw[u], hs[u])
+                product(banks[bank][:, k * (b - a) : (k + 1) * (b - a)], w2[:, e, :], s2[:, e, :], block, hw[u], hs[u][:])
 
         def gated(dest, u, bank):
             a, b = units[u]
             count = 4 * P // (b - a)
             nc.vector.tensor_tensor(
-                dest[:],
+                dest,
                 banks[bank][:].rearrange("p (k s) -> p k s", k=count),
                 gate_t[:, a:b].unsqueeze(1).to_broadcast([P, count, b - a]),
                 MULT,
@@ -155,10 +156,8 @@ def tile_moe_two_mlp_relu2_kernel(tc, xT, w1_words, w1_scales, w2_words, w2_scal
             values = y[u][:, i, :] if u < 2 else y_late[i // 2][:, i % 2, :]
             if i >= 2:
                 nc.scalar.activation(places, values, COPY)
-            elif u == 2:
-                nc.vector.tensor_tensor(places, values, gate_t[:, a:b], MULT)
             else:
-                nc.vector.tensor_copy(places, values)
+                nc.vector.tensor_tensor(places, values, gate_t[:, a:b], MULT)
             if u == 2:
                 nc.sync.dma_start(out[i * P : (i + 1) * P, :], win[i][:])
 
@@ -192,24 +191,24 @@ def tile_moe_two_mlp_relu2_kernel(tc, xT, w1_words, w1_scales, w2_words, w2_scal
         nc.vector.tensor_scalar_max(rows(1), woven(1), 0.0)
         quantize(hw[0][:], hs[0][:], hg[0][:])
         second(0, range(4), 4)
-        nc.scalar.activation(rows(2), woven(2), RELU)
-        nc.scalar.activation(hg[1][:], r[1][:], SQUARE)
-        nc.vector.tensor_scalar_max(rows(3), woven(3), 0.0)
+        nc.vector.tensor_tensor(hg[1][:], r[1][:], r[1][:], MULT)
+        for g in range(2, 4):
+            nc.scalar.activation(rows(g), woven(g), RELU)
         for g in range(2, 4):
             nc.scalar.activation(hg_late[:, g - 2, :], r[g][:], SQUARE)
         quantize(hw[1][:], hs[1][:], hg[1][:])
         second(1, range(4), 5)
         gated(y[0], 0, 4)
-        scatter(0, 0)
+        gated(y[1], 1, 5)
         quantize(hw[2][:], hs[2][:], hg_late[:].rearrange("p g x -> p (g x)"))
         second(2, range(2), 6)
         second(2, range(2, 4), 7)
-        gated(y[1], 1, 5)
-        scatter(0, 2)
-        scatter(0, 3)
-        scatter(0, 1)
-        nc.scalar.copy(y_late[0][:].rearrange("p k s -> p (k s)"), banks[6][:])
-        gated(y_late[1], 2, 7)
-        for u in range(1, 3):
-            for i in (2, 0, 3, 1):
+        for u in range(2):
+            for i in (2, 3):
                 scatter(u, i)
+        nc.vector.tensor_copy(win[0][:].indirect(dst_t[:, 0 : C // 16]), y_early[:, 0, :])
+        gated(y_late[1][:], 2, 7)
+        nc.vector.tensor_copy(win[1][:].indirect(dst_t[:, 0 : C // 16]), y_early[:, 1, :])
+        nc.scalar.copy(y_late[0][:].rearrange("p k s -> p (k s)"), banks[6][:])
+        for i in (2, 0, 3, 1):
+            scatter(2, i)

@@ -45,13 +45,11 @@ def tile_moe_two_mlp_relu2_kernel(tc, xT, w1_words, w1_scales, w2_words, w2_scal
             )
 
         x_rows = xT.rearrange("(p j) w -> p j w", j=4)
-        for q in range(2):
-            load_scales(nc.scalar, s1_raw, w1_scales, q)
         nc.sync.dma_start(w1_raw[0][:].bitcast(I32), w1_words[0, 0].bitcast(I32))
         nc.sync.dma_start(offs_t[:], offs)
         for j in range(4):
             nc.sync.dma_start(planes[j][:], x_rows[:, j, :])
-        for q in range(2, 4):
+        for q in range(4):
             load_scales(nc.sync, s1_raw, w1_scales, q)
         nc.sync.dma_start(w1_raw[1][:].bitcast(I32), w1_words[1, 0].bitcast(I32))
         nc.sync.dma_start(w2[:].bitcast(I32), w2_words[:, 0].rearrange("e p b -> p e b").bitcast(I32))

@@ -36,6 +36,10 @@ def tile_moe_two_mlp_relu2_kernel(tc, xT, w1_words, w1_scales, w2_words, w2_scal
         planes = [keep.tile([P, T], F32, name=f"plane{j}", align_bytes=64) for j in range(4)]
         gate_t = keep.tile([P, E * C], F32, name="gate_t")
 
+        warm = keep.tile([P, 16], F32, name="warm")
+        nc.gpsimd.memset(warm[:, 0:1], 0.0)
+        nc.scalar.activation(warm[:, 8:9], warm[:, 0:1], COPY)
+
         nc.gpsimd.memset(s1_raw[:].rearrange("p e i -> p (e i)").bitcast(I32), 0)
 
         def load_scales(queue, tile, scales, q):
@@ -45,10 +49,11 @@ def tile_moe_two_mlp_relu2_kernel(tc, xT, w1_words, w1_scales, w2_words, w2_scal
             )
 
         x_rows = xT.rearrange("(p j) w -> p j w", j=4)
-        nc.sync.dma_start(w1_raw[0][:].bitcast(I32), w1_words[0, 0].bitcast(I32))
         nc.sync.dma_start(offs_t[:], offs)
-        for j in range(4):
+        for j in range(3):
             nc.sync.dma_start(planes[j][:], x_rows[:, j, :])
+        nc.sync.dma_start(w1_raw[0][:].bitcast(I32), w1_words[0, 0].bitcast(I32))
+        nc.sync.dma_start(planes[3][:], x_rows[:, 3, :])
         for q in range(4):
             load_scales(nc.sync, s1_raw, w1_scales, q)
         nc.sync.dma_start(w1_raw[1][:].bitcast(I32), w1_words[1, 0].bitcast(I32))
@@ -80,10 +85,10 @@ def tile_moe_two_mlp_relu2_kernel(tc, xT, w1_words, w1_scales, w2_words, w2_scal
         banks = [psum.tile([P, 4 * P], F32, name=f"bank{i}") for i in range(8)]
         units = ((0, P), (P, C), (C, T))
 
-        def permute_words(e, copy, a, b):
-            copy(
-                w1[e][:].bitcast(U16).rearrange("p (t m) -> p t m", t=4)[:, a:b, :],
-                w1_raw[e][:].bitcast(U16).rearrange("p (m t) -> p t m", t=4)[:, a:b, :],
+        def permute_words(e):
+            nc.vector.tensor_copy(
+                w1[e][:].bitcast(U16).rearrange("p (t m) -> p t m", t=4),
+                w1_raw[e][:].bitcast(U16).rearrange("p (m t) -> p t m", t=4),
             )
 
         def permute_scales(e):
@@ -159,8 +164,6 @@ def tile_moe_two_mlp_relu2_kernel(tc, xT, w1_words, w1_scales, w2_words, w2_scal
             if u == 2:
                 nc.sync.dma_start(out[i * P : (i + 1) * P, :], win[i][:])
 
-        permute_words(0, nc.scalar.copy, 0, 2)
-        permute_words(0, nc.vector.tensor_copy, 2, 4)
         for j in range(2):
             gather(j, 0, C, True)
             gather(j, C, T, False)
@@ -168,6 +171,7 @@ def tile_moe_two_mlp_relu2_kernel(tc, xT, w1_words, w1_scales, w2_words, w2_scal
         gather(2, P, C, False)
         gather(2, C, T, False)
         interleave(0, 3)
+        permute_words(0)
         nc.vector.tensor_copy(xg[0][:, :, 3], planes[3][:].indirect(offs_t[:, 0 : P // 16]))
         gather(3, P, C, False)
         gather(3, C, T, False)
@@ -177,7 +181,7 @@ def tile_moe_two_mlp_relu2_kernel(tc, xT, w1_words, w1_scales, w2_words, w2_scal
         interleave(1)
         interleave(2)
         first(1)
-        permute_words(1, nc.vector.tensor_copy, 0, 4)
+        permute_words(1)
         interleave(3)
         first(2)
         first(3)

@@ -162,7 +162,8 @@ def tile_moe_two_mlp_relu2_kernel(tc, xT, w1_words, w1_scales, w2_words, w2_scal
             else:
                 nc.vector.tensor_tensor(places, values, gate_t[:, a:b], MULT)
             if u == 2:
-                nc.sync.dma_start(out[i * P : (i + 1) * P, :], win[i][:])
+                queue = nc.scalar if i == 3 else nc.sync
+                queue.dma_start(out[i * P : (i + 1) * P, :], win[i][:])
 
         for j in range(2):
             gather(j, 0, C, True)

@@ -77,7 +77,8 @@ def tile_moe_two_mlp_relu2_kernel(tc, xT, w1_words, w1_scales, w2_words, w2_scal
         hw = [keep.tile([P, P], U32, name=f"hw{u}", align_bytes=64) for u in range(2)]
         hw.append(shared.tile([P, C], U32, name="hw2", align_bytes=64, offset=6144))
         hs = [keep.tile([P, w], U8, name=f"hs{u}", align_bytes=64) for u, w in enumerate((P, P, C))]
-        y_early = keep.tile([P, 4, C], F32, name="y_early", align_bytes=64)
+        y_early = keep.tile([P, 3, C], F32, name="y_early", align_bytes=64)
+        y_plain = keep.tile([P, C], F32, name="y_plain", align_bytes=64)
         y = [y_early[:, :, P * u : P * (u + 1)] for u in range(2)]
         y_late = [keep.tile([P, 2, C], F32, name=f"y_late{half}", align_bytes=64) for half in range(2)]
         win = [keep.tile([P, T], F32, name=f"win{i}") for i in (0, 2, 3)]
@@ -145,10 +146,10 @@ def tile_moe_two_mlp_relu2_kernel(tc, xT, w1_words, w1_scales, w2_words, w2_scal
 
         def gated(dest, u, bank):
             a, b = units[u]
-            count = 4 * P // (b - a)
+            count = dest.shape[1]
             nc.vector.tensor_tensor(
                 dest,
-                banks[bank][:].rearrange("p (k s) -> p k s", k=count),
+                banks[bank][:, 0 : count * (b - a)].rearrange("p (k s) -> p k s", k=count),
                 gate_t[:, a:b].unsqueeze(1).to_broadcast([P, count, b - a]),
                 MULT,
             )
@@ -156,7 +157,7 @@ def tile_moe_two_mlp_relu2_kernel(tc, xT, w1_words, w1_scales, w2_words, w2_scal
         def scatter(u, i):
             a, b = units[u]
             places = win[i][:].indirect(dst_t[:, a // 16 : b // 16])
-            values = y[u][:, i, :] if u < 2 else y_late[i // 2][:, i % 2, :]
+            values = y[u][:, i - 1, :] if u < 2 else y_late[i // 2][:, i % 2, :]
             if i >= 2:
                 nc.scalar.activation(places, values, COPY)
             else:
@@ -193,14 +194,16 @@ def tile_moe_two_mlp_relu2_kernel(tc, xT, w1_words, w1_scales, w2_words, w2_scal
             nc.scalar.activation(hg[0][:, C * half : C * (half + 1)], r[0][:, C * half : C * (half + 1)], SQUARE)
         nc.vector.tensor_scalar_max(rows(1), woven(1), 0.0)
         quantize(hw[0][:], hs[0][:], hg[0][:])
-        second(0, range(4), 4)
+        second(0, (0, 2, 3), 4)
+        product(banks[0][:, 0:P], w2[:, 0, :], s2[:, 0, :], 1, hw[0], hs[0][:])
         nc.vector.tensor_tensor(hg[1][:], r[1][:], r[1][:], MULT)
         for g in range(2, 4):
             nc.scalar.activation(rows(g), woven(g), RELU)
         for g in range(2, 4):
             nc.scalar.activation(hg_late[:, g - 2, :], r[g][:], SQUARE)
         quantize(hw[1][:], hs[1][:], hg[1][:])
-        second(1, range(4), 5)
+        second(1, (0, 2, 3), 5)
+        product(banks[0][:, P:C], w2[:, 0, :], s2[:, 0, :], 1, hw[1], hs[1][:])
         gated(y[0], 0, 4)
         gated(y[1], 1, 5)
         quantize(hw[2][:], hs[2][:], hg_late[:].rearrange("p g x -> p (g x)"))
@@ -209,9 +212,11 @@ def tile_moe_two_mlp_relu2_kernel(tc, xT, w1_words, w1_scales, w2_words, w2_scal
         for u in range(2):
             for i in (2, 3):
                 scatter(u, i)
+            if u == 0:
+                nc.scalar.copy(y_plain[:], banks[0][:, 0:C])
         nc.vector.tensor_copy(win[0][:].indirect(dst_t[:, 0 : C // 16]), y_early[:, 0, :])
         gated(y_late[1][:], 2, 7)
-        nc.vector.tensor_copy(win[1][:].indirect(dst_t[:, 0 : C // 16]), y_early[:, 1, :])
+        nc.vector.tensor_tensor(win[1][:].indirect(dst_t[:, 0 : C // 16]), y_plain[:], gate_t[:, 0:C], MULT)
         nc.scalar.copy(y_late[0][:].rearrange("p k s -> p (k s)"), banks[6][:])
         for i in (2, 0, 3, 1):
             scatter(2, i)

@@ -74,7 +74,10 @@ def tile_moe_two_mlp_relu2_kernel(tc, xT, w1_words, w1_scales, w2_words, w2_scal
         r.insert(1, shared.tile([P, 4 * P], F32, name="r1", align_bytes=64, offset=10240))
         hg = [shared.tile([P, 4 * P], BF16, name=f"hg{g}", align_bytes=64, offset=8192 + 1024 * g) for g in range(2)]
         hg_late = shared.tile([P, 2, 4 * P], BF16, name="hg_late", align_bytes=64, offset=4096)
-        hw = [keep.tile([P, P], U32, name=f"hw{u}", align_bytes=64) for u in range(2)]
+        hw = [
+            keep.tile([P, P], U32, name="hw0", align_bytes=64),
+            shared.tile([P, P], U32, name="hw1", align_bytes=64, offset=6144),
+        ]
         hw.append(shared.tile([P, C], U32, name="hw2", align_bytes=64, offset=6144))
         hs = [keep.tile([P, w], U8, name=f"hs{u}", align_bytes=64) for u, w in enumerate((P, P, C))]
         y_early = keep.tile([P, 3, C], F32, name="y_early", align_bytes=64)
@@ -84,6 +87,7 @@ def tile_moe_two_mlp_relu2_kernel(tc, xT, w1_words, w1_scales, w2_words, w2_scal
         win = [keep.tile([P, T], F32, name=f"win{i}") for i in (0, 2, 3)]
         win.insert(1, shared.tile([P, T], F32, name="win1", align_bytes=64, offset=6144))
         banks = [psum.tile([P, 4 * P], F32, name=f"bank{i}") for i in range(8)]
+        share = 160
         units = ((0, P), (P, C), (C, T))
 
         def permute_words(e):
@@ -199,8 +203,9 @@ def tile_moe_two_mlp_relu2_kernel(tc, xT, w1_words, w1_scales, w2_words, w2_scal
         nc.vector.tensor_tensor(hg[1][:], r[1][:], r[1][:], MULT)
         for g in range(2, 4):
             nc.scalar.activation(rows(g), woven(g), RELU)
-        for g in range(2, 4):
-            nc.scalar.activation(hg_late[:, g - 2, :], r[g][:], SQUARE)
+        nc.vector.tensor_tensor(hg_late[:, 0, 0:share], r[2][:, 0:share], r[2][:, 0:share], MULT)
+        nc.scalar.activation(hg_late[:, 0, share:], r[2][:, share:], SQUARE)
+        nc.scalar.activation(hg_late[:, 1, :], r[3][:], SQUARE)
         quantize(hw[1][:], hs[1][:], hg[1][:])
         second(1, (0, 2, 3), 5)
         product(banks[0][:, P:C], w2[:, 0, :], s2[:, 0, :], 1, hw[1], hs[1][:])

from contextlib import ExitStack

import concourse.mybir as mybir

F32 = mybir.dt.float32
BF16 = mybir.dt.bfloat16
I32 = mybir.dt.int32
U32 = mybir.dt.uint32
U16 = mybir.dt.uint16
U8 = mybir.dt.uint8
FP8X4 = mybir.dt.float8_e4m3fn_x4
FP4X4 = mybir.dt.float4_e2m1fn_x4
MULT = mybir.AluOpType.mult
COPY = mybir.ActivationFunctionType.Copy
RELU = mybir.ActivationFunctionType.Relu
SQUARE = mybir.ActivationFunctionType.Square

P = 128
K, T, E, C, H, N = 512, 512, 2, 256, 512, 512
FLOPS = 2 * E * C * H * (K + N)


def tile_moe_two_mlp_relu2_kernel(tc, xT, w1_words, w1_scales, w2_words, w2_scales, gate, offs, dst, out):
    nc = tc.nc
    with ExitStack() as ctx:
        keep = ctx.enter_context(tc.tile_pool(name="keep", bufs=1))
        shared = ctx.enter_context(tc.tile_pool(name="shared", bufs=1))
        psum = ctx.enter_context(tc.psum_pool(name="psum", bufs=1))

        offs_t = keep.tile([P, T // 16], U16, name="offs_t")
        dst_t = keep.tile([P, T // 16], U16, name="dst_t")
        s1_raw = keep.tile([P, E, H], U8, name="s1_raw", align_bytes=64)
        s2 = keep.tile([P, E, N], U8, name="s2", align_bytes=64)
        w1_raw = [keep.tile([P, 2 * H], U8, name=f"w1_raw{e}", align_bytes=64) for e in range(E)]
        w2 = keep.tile([P, E, 2 * N], U8, name="w2", align_bytes=64)
        planes = [keep.tile([P, T], F32, name=f"plane{j}", align_bytes=64) for j in range(4)]
        gate_t = keep.tile([P, E * C], F32, name="gate_t")

        warm = keep.tile([P, 16], F32, name="warm")
        nc.gpsimd.memset(warm[:, 0:1], 0.0)
        nc.scalar.activation(warm[:, 8:9], warm[:, 0:1], COPY)

        nc.gpsimd.memset(s1_raw[:].rearrange("p e i -> p (e i)").bitcast(I32), 0)

        def load_scales(queue, tile, scales, q):
            queue.dma_start(
                tile[32 * q : 32 * q + 4].bitcast(I32),
                scales[:, 0, 4 * q : 4 * q + 4, :].rearrange("e q i -> q e i").bitcast(I32),
            )

        x_rows = xT.rearrange("(p j) w -> p j w", j=4)
        nc.sync.dma_start(offs_t[:], offs)
        for j in range(3):
            nc.sync.dma_start(planes[j][:], x_rows[:, j, :])
        nc.sync.dma_start(w1_raw[0][:].bitcast(I32), w1_words[0, 0].bitcast(I32))
        nc.sync.dma_start(planes[3][:], x_rows[:, 3, :])
        for q in range(4):
            load_scales(nc.sync, s1_raw, w1_scales, q)
        nc.sync.dma_start(w1_raw[1][:].bitcast(I32), w1_words[1, 0].bitcast(I32))
        nc.sync.dma_start(w2[:].bitcast(I32), w2_words[:, 0].rearrange("e p b -> p e b").bitcast(I32))
        for q in range(4):
            load_scales(nc.sync, s2, w2_scales, q)
        nc.sync.dma_start(gate_t[:], gate[0:P, :])
        nc.sync.dma_start(dst_t[:], dst)

        w1 = [keep.tile([P, 2 * H], U8, name=f"w1_{e}", align_bytes=64) for e in range(E)]
        s1 = [keep.tile([P, H], U8, name=f"s1_{e}", align_bytes=64) for e in range(E)]
        picked = [keep.tile([P, 4, C], BF16, name=f"picked{e}", align_bytes=64) for e in range(E)]
        xg = [shared.tile([P, P, 4], BF16, name=f"xg{g}", align_bytes=64, offset=at) for g, at in enumerate((2048, 12288 - 64, 1024, 12288 - 64))]
        xw = [keep.tile([P, P], U32, name=f"xw{g}", align_bytes=64) for g in range(4)]
        xs_first = keep.tile([P, P], U8, name="xs_first", align_bytes=64)
        xs = [xs_first[:]] + [s1_raw[:, 0, P * g : P * (g + 1)] for g in range(3)]
        r = [keep.tile([P, 4 * P], F32, name=f"r{g}", align_bytes=64) for g in (0, 2, 3)]
        r.insert(1, shared.tile([P, 4 * P], F32, name="r1", align_bytes=64, offset=10240))
        hg = [shared.tile([P, 4 * P], BF16, name=f"hg{g}", align_bytes=64, offset=8192 + 1024 * g) for g in range(2)]
        hg_late = shared.tile([P, 2, 4 * P], BF16, name="hg_late", align_bytes=64, offset=4096)
        hw = [
            keep.tile([P, P], U32, name="hw0", align_bytes=64),
            shared.tile([P, P], U32, name="hw1", align_bytes=64, offset=6144),
        ]
        hw.append(shared.tile([P, C], U32, name="hw2", align_bytes=64, offset=6144))
        hs = [keep.tile([P, w], U8, name=f"hs{u}", align_bytes=64) for u, w in enumerate((P, P, C))]
        y_early = keep.tile([P, 3, C], F32, name="y_early", align_bytes=64)
        y_plain = keep.tile([P, C], F32, name="y_plain", align_bytes=64)
        y = [y_early[:, :, P * u : P * (u + 1)] for u in range(2)]
        y_late = [keep.tile([P, 2, C], F32, name=f"y_late{half}", align_bytes=64) for half in range(2)]
        win = [keep.tile([P, T], F32, name=f"win{i}") for i in (0, 2, 3)]
        win.insert(1, shared.tile([P, T], F32, name="win1", align_bytes=64, offset=6144))
        banks = [psum.tile([P, 4 * P], F32, name=f"bank{i}") for i in range(8)]
        share = 160
        units = ((0, P), (P, C), (C, T))

        def permute_words(e):
            nc.vector.tensor_copy(
                w1[e][:].bitcast(U16).rearrange("p (t m) -> p t m", t=4),
                w1_raw[e][:].bitcast(U16).rearrange("p (m t) -> p t m", t=4),
            )

        def permute_scales(e):
            nc.vector.tensor_copy(
                s1[e][:].rearrange("p (t m) -> p t m", t=4),
                s1_raw[:, e, :].rearrange("p (m t) -> p t m", t=4),
            )

        def gather(j, a, b, on_vector):
            dest = picked[a // C][:, j, a % C : a % C + b - a]
            source = planes[j][:].indirect(offs_t[:, a // 16 : b // 16])
            if on_vector:
                nc.vector.tensor_copy(dest, source)
            else:
                nc.scalar.activation(dest, source, COPY)

        def interleave(g, count=4):
            copy = nc.scalar.copy if g in (1, 2) else nc.vector.tensor_copy
            copy(
                xg[g][:, :, 0:count].rearrange("p (c i) j -> p c j i", i=4),
                picked[g // 2][:, 0:count, P * (g % 2) : P * (g % 2 + 1)].rearrange("p j (c i) -> p c j i", i=4),
            )

        def quantize(codes, scales, values):
            nc.vector.quantize_mx(out=codes.bitcast(FP8X4), scales=scales, in_=values)

        def product(dest, weights, weight_scales, block, codes, scales):
            nc.tensor.matmul_mx(
                out=dest,
                lhsT=weights[:, 256 * block : 256 * (block + 1)].bitcast(FP4X4),
                lhsT_scale=weight_scales[:, P * block : P * (block + 1)],
                rhs=codes[:].bitcast(FP8X4),
                rhs_scale=scales,
                start=True,
                stop=True,
            )

        def first(g):
            quantize(xw[g][:], xs[g], xg[g][:].rearrange("p s j -> p (s j)"))
            for t in range(4):
                product(banks[g][:, P * t : P * (t + 1)], w1[g // 2], s1[g // 2], t, xw[g], xs[g])

        def woven(g):
            return banks[g][:].rearrange("p (t s) -> p s t", t=4)

        def rows(g):
            return r[g][:].rearrange("p (s t) -> p s t", t=4)

        def second(u, blocks, bank):
            a, b = units[u]
            e = a // C
            for k, block in enumerate(blocks):
                product(banks[bank][:, k * (b - a) : (k + 1) * (b - a)], w2[:, e, :], s2[:, e, :], block, hw[u], hs[u][:])

        def gated(dest, u, bank):
            a, b = units[u]
            count = dest.shape[1]
            nc.vector.tensor_tensor(
                dest,
                banks[bank][:, 0 : count * (b - a)].rearrange("p (k s) -> p k s", k=count),
                gate_t[:, a:b].unsqueeze(1).to_broadcast([P, count, b - a]),
                MULT,
            )

        def scatter(u, i):
            a, b = units[u]
            places = win[i][:].indirect(dst_t[:, a // 16 : b // 16])
            values = y[u][:, i - 1, :] if u < 2 else y_late[i // 2][:, i % 2, :]
            if i >= 2:
                nc.scalar.activation(places, values, COPY)
            else:
                nc.vector.tensor_tensor(places, values, gate_t[:, a:b], MULT)
            if u == 2:
                queue = nc.scalar if i == 3 else nc.sync
                queue.dma_start(out[i * P : (i + 1) * P, :], win[i][:])

        for j in range(2):
            gather(j, 0, C, True)
            gather(j, C, T, False)
        gather(2, 0, P, True)
        gather(2, P, C, False)
        gather(2, C, T, False)
        interleave(0, 3)
        permute_words(0)
        nc.vector.tensor_copy(xg[0][:, :, 3], planes[3][:].indirect(offs_t[:, 0 : P // 16]))
        gather(3, P, C, False)
        gather(3, C, T, False)
        permute_scales(0)
        first(0)
        permute_scales(1)
        interleave(1)
        interleave(2)
        first(1)
        permute_words(1)
        interleave(3)
        first(2)
        first(3)

        for half in range(2):
            nc.scalar.activation(rows(0)[:, 64 * half : 64 * (half + 1), :], woven(0)[:, 64 * half : 64 * (half + 1), :], RELU)
        for half in range(2):
            nc.scalar.activation(hg[0][:, C * half : C * (half + 1)], r[0][:, C * half : C * (half + 1)], SQUARE)
        nc.vector.tensor_scalar_max(rows(1), woven(1), 0.0)
        quantize(hw[0][:], hs[0][:], hg[0][:])
        second(0, (0, 2, 3), 4)
        product(banks[0][:, 0:P], w2[:, 0, :], s2[:, 0, :], 1, hw[0], hs[0][:])
        nc.vector.tensor_tensor(hg[1][:], r[1][:], r[1][:], MULT)
        for g in range(2, 4):
            nc.scalar.activation(rows(g), woven(g), RELU)
        nc.vector.tensor_tensor(hg_late[:, 0, 0:share], r[2][:, 0:share], r[2][:, 0:share], MULT)
        nc.scalar.activation(hg_late[:, 0, share:], r[2][:, share:], SQUARE)
        nc.scalar.activation(hg_late[:, 1, :], r[3][:], SQUARE)
        quantize(hw[1][:], hs[1][:], hg[1][:])
        second(1, (0, 2, 3), 5)
        product(banks[0][:, P:C], w2[:, 0, :], s2[:, 0, :], 1, hw[1], hs[1][:])
        gated(y[0], 0, 4)
        gated(y[1], 1, 5)
        quantize(hw[2][:], hs[2][:], hg_late[:].rearrange("p g x -> p (g x)"))
        second(2, range(2), 6)
        second(2, range(2, 4), 7)
        for u in range(2):
            for i in (2, 3):
                scatter(u, i)
            if u == 0:
                nc.scalar.copy(y_plain[:], banks[0][:, 0:C])
        nc.vector.tensor_copy(win[0][:].indirect(dst_t[:, 0 : C // 16]), y_early[:, 0, :])
        gated(y_late[1][:], 2, 7)
        nc.vector.tensor_tensor(win[1][:].indirect(dst_t[:, 0 : C // 16]), y_plain[:], gate_t[:, 0:C], MULT)
        nc.scalar.copy(y_late[0][:].rearrange("p k s -> p (k s)"), banks[6][:])
        for i in (2, 0, 3, 1):
            scatter(2, i)
